import numpy as np, ml_dtypes
CORES = [23,119,17,113]
N = 4
BF = ml_dtypes.bfloat16
def gentries(a):
    return np.ascontiguousarray(a.reshape(8, 16, -1).transpose(0, 2, 1)).reshape(8, -1)
def gtable(e):
    e = np.asarray(e); return np.ascontiguousarray(e.reshape(8, -1, 16).transpose(0, 2, 1)).reshape(128, -1).astype(np.int32)
S, C, B, U, RO, Q = 4096, 4096, 192, 64, 4, 9
L = B + U
def parts(rng):
    sk = (256 * (0.25 + 0.75 * rng.random((N, 8, 1, C))) * rng.random((N, 8, 16, C))).astype(np.int64); sk = np.minimum(sk, 255); sk[..., C - 1] = 0
    oc = np.where(rng.random((N, 8, S)) < 0.05, C - 1, rng.integers(0, C - 1, (N, 8, S)))
    cv = rng.integers(0, S, (N, 8, 16, S)); cd = np.ascontiguousarray(np.argsort(rng.random((N, 8, RO, S)), axis=-1)[..., :L * 16])
    return sk, oc, cv, cd
def fill(rng, share):
    u = rng.random((N, 8, 1, RO, B)); v = rng.random((N, 8, 1, RO, B))
    h = np.where(u < share, 9 + 31 * v, np.where(u < share + 0.1, 4 + 5 * v, np.where(u < share + 0.3, 0.0, 0.2 + 3.8 * v)))
    w = rng.random((N, 8, 16, RO, B)) * (rng.random((N, 8, 16, RO, B)) < 0.7)
    return np.minimum((80 * h * w).astype(np.int64), 4096)
def sums(sk, oc, cd):
    who = np.take_along_axis(oc, cd[:, :, 0, :B * 16], 2)
    return np.add.accumulate(np.take_along_axis(sk, who[:, :, None, :], 3).reshape(N, 8, 16, B, 16), axis=4)
def heavy(rng, sk, oc, cv, cd, nd):
    own = np.arange(S); j = np.arange(B)
    for g in rng.permutation(8)[:2]:
        left = []
        for q in range(N):
            v = rng.integers(200, 256, (16, C)); v[:, C - 1] = 0; e = rng.integers(L, C - 1, S)
            st = cd[q, g, 0].reshape(L, 16); late = st[B:].reshape(-1)
            cd[q, g, 1] = np.concatenate([rng.permutation(st[:B].reshape(-1)), rng.permutation(late)])
            cv[q, g] = rng.choice(np.setdiff1d(own, late), (16, S))
            p = rng.integers(10, 16, B); before = np.add.accumulate(v[:, e[st[:B]]], axis=2)[:, j, p - 1]
            x = 208 + (-before) % 16; want = before + x
            x[rng.integers(0, 16, B), j] -= rng.integers(0, 2, B)
            v[:, :B] = x; e[st[j, p]] = j
            big = rng.permutation(B)[:U // 2]; e[st[big[U // 8:], 8:]] = C - 1
            want[:, big] = 0; want[rng.integers(0, 16, U // 2), big] = 4096
            sk[q, g] = v; oc[q, g] = e; nd[q, g] = 0; nd[q, g, :, 0] = want
            end = np.add.reduce(v[:, e[st[:B]]], axis=2); u = np.nonzero(np.any(end < want, axis=0))[0][:U]
            left.append(np.maximum(want[:, u] - end[:, u], 0))
        for q in range(N):
            w = left[q - 1]; n = w.shape[1]; k = np.arange(n); z = np.argmax(w, axis=0); top = w[z, k]
            st = cd[q, g, 1].reshape(L, 16)[B:B + n]
            line = np.add.accumulate(sk[q, g][z[:, None], oc[q, g][st]], axis=1)
            p = np.add.reduce((line < top[:, None]).astype(np.int64), axis=1)
            before = np.where(p > 0, line[k, np.maximum(p - 1, 0)], 0)
            sk[q, g, z, B + k] = top - before - k % 2; oc[q, g, st[k, p]] = B + k
def pack(sk, oc, cv, cd, nd):
    return {"skill": np.ascontiguousarray(sk.reshape(N, 128, C)).astype(np.float32).astype(BF), "occ": oc.astype(np.int32), "cover": np.ascontiguousarray(cv.reshape(N, 128, S)).astype(np.int32),
            "cards": np.stack([gtable(a.reshape(8, -1)) for a in cd]), "need": np.ascontiguousarray(nd.reshape(N, 128, RO * B)).astype(np.float32).astype(BF)}
def setup_inputs(rng):
    sk, oc, cv, cd = parts(rng)
    return pack(sk, oc, cv, cd, fill(rng, rng.choice(np.array([0.03, 0.1, 0.2, 0.3]), (N, 8, 1, 1, 1))))
def setup_inputs_room(rng):
    sk, oc, cv, cd = parts(rng); nd = np.zeros((N, 8, 16, RO, B), np.int64); pre = sums(sk, oc, cd)
    nd[:, :, :, 0] = pre[..., 0] * (rng.random((N, 8, 1, B)) < 0.5)
    for q in range(N):
        for t in range(RO):
            size = rng.permutation(np.array([0, 1, U - 1, U, U + 1, B, U, 0]))
            for g in range(8):
                n = int(size[g]); lanes = rng.permutation(B)[:n]
                nd[q, g, :, t, lanes] = rng.integers(0, 256, (n, 16)); nd[q, g, rng.integers(0, 16, n), t, lanes] = 4096
    return pack(sk, oc, cv, cd, nd)
def setup_inputs_ties(rng):
    sk, oc, cv, cd = parts(rng)
    few = rng.integers(0, 3, sk.shape) * 16; m = np.arange(8)[None, :, None, None] % 2 == 0
    sk = np.where(m, few, sk // 16 * 16) * (rng.random((N, 8, 1, C)) > 0.1); sk[..., C - 1] = 0
    nd = fill(rng, 0.05); pre = sums(sk, oc, cd)
    p = rng.choice(np.array([0, 0, 1, 3, 7, 14, 15, 15]), (N, 8, B))
    w = np.take_along_axis(pre, p[:, :, None, :, None], 4)[..., 0]
    w = w + 16 * ((np.arange(16)[None, None, :, None] == rng.integers(0, 16, (N, 8, 1, B))) & (rng.random((N, 8, 1, B)) < 0.5))
    nd[:, :, :, 0] = w * (rng.random((N, 8, 1, B)) > 0.3)
    heavy(rng, sk, oc, cv, cd, nd)
    return pack(sk, oc, cv, cd, nd)
def setup_inputs_crowd(rng):
    sk, oc, cv, cd = parts(rng); h = B // 2; sk[..., 0] = 255; own = np.arange(S); o = rng.permutation(8)
    full = np.argsort(rng.random((N, 8, B)), axis=-1)[..., :U]
    for q in range(N):
        for g in range(8):
            card = cd[q, g, 0].reshape(L, 16)
            if g == o[0] or g == o[1]:
                k = rng.permutation(np.setdiff1d(own, card[full[q, g]].reshape(-1))); a, b = k[:L], k[L:2 * L]
                mid = rng.permutation(np.setdiff1d(own, k[:2 * L]))[:14 * L].reshape(L, 14)
                cd[q, g, 1] = np.concatenate([a[:, None], mid, b[:, None]], axis=1).reshape(-1)
                v = np.clip(sk[q, g], 16, 239); v[:, :16] = rng.integers(240, 256, (16, 16)); v[:, C - 1] = 0; sk[q, g] = v
                oc[q, g, a] = rng.integers(16, C - 1, L); oc[q, g, b] = rng.integers(0, 16, L)
                c = np.repeat(own[None, :], 16, axis=0)
                if g == o[0]: c[:, a] = b[rng.integers(0, 2, (16, L))]
                else: c[:, a] = np.where(np.arange(16)[:, None] >= rng.integers(0, 16, L)[None, :], b[None, :], a[None, :])
                cv[q, g] = c
            else:
                pool = card[h:h + 16, 15]; oc[q, g, pool[:8]] = 0
                c = pool[rng.integers(0, 16, (16, S))]; kind = rng.integers(0, 5, S)
                c[:15] = np.where(kind >= 3, own, c[:15]); c[15] = np.where(kind == 4, own, c[15]); cv[q, g] = c
    nd = fill(rng, 0.05); pre = sums(sk, oc, cd)
    nd[:, :, :, 0] = pre[..., 0] * (np.arange(B) < h); nd[:, o[:2]] = 0
    for q in range(N):
        for g in o[:2]:
            z = rng.integers(0, 16, U); l = full[q, g]; nd[q, g, z, 0, l] = pre[q, g, z, l, 15] // 16 * 16 + 16
            nd[q, g, rng.integers(0, 16, B), 1, np.arange(B)] = rng.integers(1, 17, B)
    return pack(sk, oc, cv, cd, nd)
def setup_inputs_bare(rng):
    sk, oc, cv, cd = parts(rng); h = rng.permutation(8)
    oc = np.where(rng.random((N, 8, S)) < rng.choice(np.array([0.4, 0.6, 0.8]), (N, 8, 1)), C - 1, oc); oc[:, h[0]] = C - 1
    ends = np.array([0, 1, S - 2, S - 1]); cv[:, h[2]] = rng.choice(ends, (N, 16, S)); oc[:, h[2], :2] = rng.integers(0, C - 1, (N, 2)); oc[:, h[2], S - 2:] = rng.integers(0, C - 1, (N, 2))
    nd = fill(rng, 0.05) * (rng.random((N, 8, 1, RO, B)) < 0.5); nd[::2, h[1]] = 0
    return pack(sk, oc, cv, cd, nd)
def setup_inputs_spread(rng):
    sk, oc, cv, cd = parts(rng)
    sk = np.minimum((np.exp2(8.2 * rng.random((N, 8, 1, C))) * rng.random((N, 8, 16, C))).astype(np.int64), 255); sk[..., C - 1] = 0
    oc = np.where(rng.random((N, 8, S)) < 0.1, C - 1, np.minimum(((C - 1) * rng.random((N, 8, S)) ** 3).astype(np.int64), C - 2))
    cv = np.minimum((S * rng.random((N, 8, 16, S)) ** 2).astype(np.int64), S - 1)
    nd = (np.minimum(np.exp2(12.2 * rng.random((N, 8, 1, RO, B))), 4096) * rng.choice(np.array([0.0, 0.25, 0.5, 1.0]), (N, 8, 16, RO, B))).astype(np.int64)
    return pack(sk, oc, cv, cd, nd * (rng.random((N, 8, 1, RO, B)) > 0.3))
def check_inputs(d):
    bad = []
    for k, hi in (("skill", 255), ("need", 4096), ("occ", C - 1), ("cover", S - 1), ("cards", S - 1)):
        x = np.asarray(d[k]).astype(np.float64)
        if not np.all((x >= 0) & (x <= hi) & (x == np.floor(x))): bad.append("range of " + k)
    if not np.all(np.asarray(d["skill"])[:, :, C - 1].astype(np.float32) == 0): bad.append("last column of skill")
    e = np.sort(np.asarray(d["cards"]).reshape(N, 8, 16, RO, L).transpose(0, 1, 3, 2, 4).reshape(N, 8, RO, 16 * L), axis=-1)
    if np.any(e[..., 1:] == e[..., :-1]): bad.append("equal stations on the cards of a round")
    return bad
def reference(skill, occ, cover, cards, need):
    sk = skill.astype(np.float32).astype(np.int64).reshape(N, 8, 16, C); cv = cover.astype(np.int64).reshape(N, 8, 16, S)
    cd = np.stack([gentries(a) for a in cards]).astype(np.int64).reshape(N, 8, RO, L, 16); nd = need.astype(np.float32).astype(np.int64).reshape(N, 8, 16, RO, B)
    oc = np.array(occ, dtype=np.int64); arrived = np.zeros((N, 8, 16, U), np.int64)
    for t in range(RO):
        sent = np.zeros((N, 8, 16, U), np.int64)
        for r in range(N):
            w = np.concatenate([nd[r, :, :, t], arrived[r]], axis=2)
            st = cd[r, :, t]; flat = st.reshape(8, -1)
            who = np.take_along_axis(oc[r], flat, 1)
            col = np.take_along_axis(sk[r], who[:, None, :], 2).reshape(8, 16, L, 16)
            pre = np.add.accumulate(col, axis=3)
            met = np.all(pre >= w[..., None], axis=1)
            zero = np.all(w == 0, axis=1)
            leave = ~np.concatenate([zero[..., None], met[..., :15]], axis=2)
            unmet = ~met[..., 15]; before = np.add.accumulate(unmet.astype(np.int64), axis=1) - unmet
            rest = np.maximum(w - pre[..., 15], 0); g, l = np.nonzero(unmet & (before < U))
            sent[(r + 1) % N][g, :, before[g, l]] = rest[g, :, l]
            np.put_along_axis(oc[r], flat, np.where(leave.reshape(8, -1), C - 1, who), 1)
            s = st[..., 0]; lost = leave[..., 0] & (who.reshape(8, L, 16)[..., 0] != C - 1)
            m = np.take_along_axis(cv[r], s[:, None, :], 2)
            a = np.take_along_axis(oc[r], m.reshape(8, -1), 1)
            ka = np.take_along_axis(sk[r], a[:, None, :], 2).reshape(8, 16, 16, L)
            a = a.reshape(8, 16, L); good = np.add.reduce((ka >= col[:, :, None, :, 0]).astype(np.int64), axis=1)
            fit = (a != C - 1) & (good >= Q); ok = lost & np.any(fit, axis=1)
            i = np.argmax(fit, axis=1)[:, None, :]
            src = np.take_along_axis(m, i, 1)[:, 0]; new = np.take_along_axis(a, i, 1)[:, 0]
            for g in range(8):
                lanes = np.nonzero(ok[g])[0]
                out, at = np.unique(src[g, lanes], return_index=True); lanes = lanes[at]
                oc[r, g, s[g, lanes]] = new[g, lanes]; oc[r, g, out] = C - 1
        arrived = sent
    return {"y": oc.astype(np.float32)}

@@ -1,0 +1,480 @@
+from concourse.mybir import AluOpType, ActivationFunctionType
+
+OP = AluOpType
+FN = ActivationFunctionType
+K0, TOL = 14, 7
+CH = [(0, 32), (32, 32), (64, 64), (128, 64), (192, 64)]
+VL = 160
+FG = [(0, 64), (64, 64), (128, 32)]
+SG3 = [(160, 32), (192, 32), (224, 32)]
+PART = [("P6", 0, 64), ("P7", 64, 64), ("P6", 128, 32), ("P4", 160, 96)]
+STEP1 = "v0 a1 b0 a2 b1 n3 s0 s1 l0 l1 n2 r32 t0 t1 s2 v3 l2 q0 n3 s3 t2 v4 l3 s4 q1 t3 l4"
+STEP3 = "u0 g0 g1 v0 c0 s0 g2 v1 f0 o0 c1 s1 s2 m0 v2 c3 f1 o1 c2 L0 p0 f3 o3 P0 f2 o2"
+
+_sb = {
+    "OT0": (128, "int32"), "OT1": (128, "int32"), "OH0": (128, "float16"), "OH1": (128, "float16"), "OLU": (256, "uint16"),
+    "OCN": (256, "int32"), "OCH": (256, "float16"),
+    "SK": (4096, "bfloat16"), "COV": (4096, "int32"), "CI": (1024, "int32"), "CU": (1024, "uint16"), "CF": (1024, "float16"),
+    "ND": (768, "bfloat16"), "NN": (768, "bfloat16"), "LS": (128, "uint16"), "KS": (64, "float32"),
+    "WA": (4608, "float32"), "WB": (4608, "float32"), "OO": (4608, "float32"),
+    "ONE": (2048, "bfloat16"), "I": (128, "bfloat16"), "NI": (128, "bfloat16"), "B": (128, "bfloat16"), "BB": (128, "bfloat16"),
+    "PX": (2048, "bfloat16"), "ZB": (144, "bfloat16"), "Z0": (144, "bfloat16"), "Z15": (144, "bfloat16"), "Z8": (144, "bfloat16"),
+    "G8": (8, "bfloat16"), "G15": (8, "bfloat16"),
+    "TRI": (128, "bfloat16"), "UP": (128, "bfloat16"), "UN": (128, "bfloat16"), "W3": (128, "bfloat16"),
+    "PI": (1, "int32"), "PA": (1, "int32"), "XC": (1, "float32"), "ZR": (256, "float32"), "LY": (16, "float32"), "KM": (16, "float32"),
+    "KD": (32, "float32"), "DM": (1024, "bfloat16"), "ON16": (16, "float32"), "ZZ": (256, "bfloat16"),
+    "D0": (528, "bfloat16"), "D1": (528, "bfloat16"), "D2": (1040, "bfloat16"), "D3": (1040, "bfloat16"), "D4": (1040, "float32"),
+    "R": (3072, "bfloat16"), "RF": (1024, "float32"), "IN1": (4096, "bfloat16"), "X": (4096, "float32"),
+    "NA": (64, "bfloat16"), "AR": (64, "float32"), "RR": (256, "float32"), "U01": (256, "bfloat16"), "UL": (16, "bfloat16"),
+    "UK": (16, "float32"), "UK2": (16, "float32"), "CY": (16, "float32"), "SP": (16, "float32"), "OF": (16, "float32"), "OU": (16, "uint16"),
+    "BS": (512, "bfloat16"), "BT": (256, "float32"), "BRF": (VL * 16, "float32"), "BRH": (4096 - VL * 16, "bfloat16"),
+    "CLF": (256, "float16"), "CLU": (256, "uint16"), "IN3": (VL * 16, "bfloat16"), "GA": (4096 - VL * 16, "bfloat16"), "SGN": (4096 - VL * 16, "bfloat16"),
+    "L1": (16, "float32"), "L2": (16, "float32"), "LOST": (16, "float32"),
+    "F": (256, "bfloat16"), "SM": (512, "float16"), "CR": (256, "float16"), "CLI": (16, "float32"), "OKL": (16, "float32"), "OB": (16, "float32"),
+    "CLM": (16, "float32"), "R2": (32, "float32"), "R3": (32, "float32"), "R4": (32, "float32"), "OFS": (32, "uint16"), "MLU": (16, "uint16"),
+    "VB": (512, "float32"), "OV": (256, "float32"),
+    "DL": (256, "bfloat16"), "ZF": (256, "float32"), "OFN": (256, "float32"), "OI": (256, "int32"), "EF": (256, "float32"), "YF": (256, "float32"),
+}
+SCRATCH = {k: ("sbuf", [128, n], d) for k, (n, d) in _sb.items()}
+SCRATCH["E"] = ("sbuf", [128, 16, 256], "bfloat16")
+SCRATCH["MK"] = ("sbuf", [128, 16, 16], "bfloat16")
+SCRATCH["MD"] = ("sbuf", [128, 16, 16], "bfloat16")
+for _t in range(3):
+    SCRATCH["SW%d" % _t] = ("sbuf", [128, 512], "int32")
+    SCRATCH["AV%d" % _t] = ("sbuf", [128, 64], "int32")
+SCRATCH["TA"] = ("psum", [128, 1024], "float32")
+SCRATCH["TB"] = ("psum", [128, 1024], "float32")
+for _t in range(4, 8):
+    SCRATCH["P%d" % _t] = ("psum", [128, 512], "float32")
+PS = ("TA", "TB", "P4", "P5", "P6", "P7")
+SEMAPHORES = ["cV", "cS", "cT", "cG"] + ["arr%d" % t for t in range(3)] + ["loc%d" % t for t in range(3)] + ["d%d" % k for k in range(24)]
+
+
+def rank_program(g, core, T, topo):
+    rank = T.rank_of(core)
+    if rank is None:
+        return
+    queues = {"V": g.vector, "S": g.scalar, "T": g.tensor, "G": g, "Y": g.sync}
+    count = {"cV": 0, "cS": 0, "cT": 0, "cG": 0}
+    known = {q: {} for q in queues}
+    clocks = {}
+    log = {}
+    nd, nn = [0], [0]
+
+    def A(name, a=0, b=None, s=1):
+        n = SCRATCH[name][1][1]
+        b = n if b is None else b
+        ap = T[name][:, a:b] if s == 1 else T[name][:, a:b:s]
+        return (ap, [(name, a, b, s)])
+
+    def ind(win, off):
+        return (win[0].indirect(off[0]), win[1] + off[1])
+
+    def keys(name, a, b, s=1):
+        if name in PS:
+            return [("%s.%d" % (name, k), 0, 512, 1, True) for k in range(a // 512, (b - 1) // 512 + 1)]
+        return [(name, a, b, s, False)]
+
+    def apart(a, b, s, x, y, z):
+        return x >= b or y <= a or (s == z and s > 1 and (a - x) % s != 0)
+
+    def need_event(q, ev):
+        if known[q].get(ev[0], 0) >= ev[1]:
+            return
+        queues[q].wait_ge(T.sem[ev[0]], ev[1])
+        k = known[q]
+        for s, v in clocks.get(ev, {}).items():
+            if k.get(s, 0) < v:
+                k[s] = v
+        if k.get(ev[0], 0) < ev[1]:
+            k[ev[0]] = ev[1]
+
+    def deps(q, reads, writes):
+        out = {}
+        for ops, w in ((reads, False), (writes, True)):
+            for o in ops:
+                for region in o[1]:
+                    for key, lo, hi, st, bank in keys(*region):
+                        for (x, y, ev, eq, ew, z) in log.get(key, []):
+                            if apart(lo, hi, st, x, y, z) or (eq == q == "T" and bank):
+                                continue
+                            if (ew or w or (bank and eq != q)) and out.get(ev[0], 0) < ev[1]:
+                                out[ev[0]] = ev[1]
+        return out
+
+    def record(q, ev, reads, writes):
+        for ops, w in ((reads, False), (writes, True)):
+            for o in ops:
+                for region in o[1]:
+                    for key, lo, hi, st, bank in keys(*region):
+                        keep = []
+                        for r in log.get(key, []):
+                            inside = lo <= r[0] and r[1] <= hi and (st == 1 or (st == r[5] and (lo - r[0]) % st == 0))
+                            if inside and r[3] == q and r[2][0] == ev[0] and (w or not r[4]):
+                                continue
+                            keep.append(r)
+                        keep.append((lo, hi, ev, q, w, st))
+                        log[key] = keep
+
+    def waits(q, reads, writes):
+        for s, v in sorted(deps(q, reads, writes).items(), key=lambda e: -e[1]):
+            need_event(q, (s, v))
+
+    def emit(q, fn, reads, writes):
+        waits(q, reads, writes)
+        sem = "c" + q
+        inst = fn()
+        count[sem] += 1
+        inst.then_inc(T.sem[sem], 1)
+        ev = (sem, count[sem])
+        clocks[ev] = dict(known[q])
+        record(q, ev, reads, writes)
+
+    def dma(q, out, in_, reads, writes):
+        waits(q, reads, writes)
+        ev = ("d%d" % nd[0], 16)
+        nd[0] += 1
+        queues[q].dma_start(out, in_).then_inc(T.sem[ev[0]], 16)
+        clocks[ev] = dict(known[q])
+        record("dma%d" % nd[0], ev, reads, writes)
+        return ev
+
+    V, S, TE = g.vector, g.scalar, g.tensor
+
+    def vts(out, i, s1, op0, s2=None, op1=None):
+        rd = [i] + [s for s in (s1, s2) if isinstance(s, tuple)]
+        a1 = s1[0] if isinstance(s1, tuple) else s1
+        a2 = s2[0] if isinstance(s2, tuple) else s2
+        if op1 is None:
+            emit("V", lambda: V.tensor_scalar(out[0], i[0], a1, None, op0), rd, [out])
+        else:
+            emit("V", lambda: V.tensor_scalar(out[0], i[0], a1, a2, op0, op1), rd, [out])
+
+    def vtt(out, i, j, op):
+        emit("V", lambda: V.tensor_tensor(out[0], i[0], j[0], op), [i, j], [out])
+
+    def vcp(out, i):
+        emit("V", lambda: V.tensor_copy(out[0], i[0]), [i], [out])
+
+    def vms(out, c):
+        emit("V", lambda: V.memset(out[0], c), [], [out])
+
+    def scan_(out, m, d, first):
+        emit("V", lambda: V.tensor_tensor_scan(out[0], m[0], d[0], first, OP.mult, OP.add), [m, d], [out])
+
+    def act(out, i, fn, bias=0.0, scale=1.0):
+        if bias == 0.0 and scale == 1.0:
+            emit("S", lambda: S.activation(out[0], i[0], fn), [i], [out])
+        else:
+            emit("S", lambda: S.activation(out[0], i[0], fn, bias=bias, scale=scale), [i], [out])
+
+    def mm(out, l, r, start=True, stop=True):
+        emit("T", lambda: TE.matmul(out[0], l[0], r[0], start, stop), [l, r], [out])
+
+    def sel(out, i, pattern, op, fill, base, mult):
+        emit("G", lambda: g.affine_select(out[0], i[0], pattern, op, fill, base, mult), [i], [out])
+
+    def gcp(out, i, n):
+        sel(out, i, [[0, n]], OP.is_ge, 0.0, 0, 0)
+
+    def iota(out, pattern, base, mult, small=True):
+        if small:
+            emit("G", lambda: g.iota(out[0], pattern, base, mult, allow_small_or_imprecise_dtypes=True), [], [out])
+        else:
+            emit("G", lambda: g.iota(out[0], pattern, base, mult), [], [out])
+
+    def EX(name, x):
+        return A(name, 15 - x, 143 - x)
+
+    def collect(out, name, rhs):
+        for x in range(16):
+            mm(out, EX(name, x), rhs(x), x == 0, x == 15)
+
+    for h in range(2):
+        for d in range(8):
+            o = A("OT%d" % h, 16 * d, 16 * d + 16)
+            dma("Y" if h == 0 else "S", o[0], T.occ[d, 2048 * h:2048 * h + 2048], [], [o])
+    dma("S", T.SK[:, :], T.skill[:, :], [], [A("SK")])
+    dma("Y", T.CI[:, :], T.cards[:, :], [], [A("CI")])
+    dma("Y", T.ND[:, :], T.need[:, :], [], [A("ND")])
+    dma("Y", T.OCN[:, :], T.occ[:, :], [], [A("OCN")])
+    dma("Y", T.COV[:, :], T.cover[:, :], [], [A("COV")])
+
+    iota(A("PI"), [[0, 1]], 0, 1, False)
+    iota(A("ZR"), [[0, 16], [1, 16]], 0, 0)
+    iota(A("LY"), [[16, 16]], 0, 0)
+    vms(A("ONE"), 1.0)
+    for z in ("ZB", "Z0", "Z8", "Z15"):
+        vms(A(z), 0.0)
+    vms(A("DM"), 1.0)
+    vms(A("DM", 0, 1024, 16), 0.0)
+    sel(A("I"), A("ONE", 0, 128), [[-1, 128]], OP.is_equal, 0.0, 0, 1)
+    sel(A("UN"), A("ONE", 0, 128), [[-16, 8], [0, 16]], OP.is_ge, 0.0, 0, 1)
+    sel(A("B"), A("UN"), [[16, 8], [0, 16]], OP.is_ge, 0.0, 15, -1)
+    sel(A("G8"), A("ONE", 0, 8), [[-16, 8]], OP.is_equal, 0.0, 0, 1)
+    sel(A("G15"), A("ONE", 0, 8), [[-16, 8]], OP.is_equal, 0.0, -15, 1)
+    sel(A("TRI"), A("B"), [[1, 128]], OP.is_gt, 0.0, 0, -1)
+    sel(A("UP"), A("B"), [[-1, 128]], OP.is_gt, 0.0, 0, 1)
+    sel(A("PX"), A("ONE"), [[-1, 16], [-16, 8], [0, 16]], OP.is_equal, 0.0, 0, 1)
+    for t in range(3):
+        iota(A("SW%d" % t, 0, 64), [[0, 64]], 0, 0, False)
+    vms(A("VB", 256, 512), 0.0)
+    vms(A("ON16"), 1.0)
+    vms(A("ZZ"), 0.0)
+    vms(A("NA"), 0.0)
+    vts(A("PA"), A("PI"), 15, OP.bitwise_and)
+    vcp(A("XC"), A("PA"))
+    mk = (T.MK[:, :, :], [("MK", 0, 16)])
+    for y in range(16):
+        vts((T.MK[:, y, :], [("MK", y, y + 1)]), A("ZR", 0, 16), A("XC"), OP.is_gt)
+    vts(A("KD", 0, 16), A("LY"), A("XC"), OP.add)
+    vts(A("KD", 16, 32), A("KD", 0, 16), 256.0, OP.add)
+    vts(A("KM"), A("KD", 0, 16), 256.0, OP.add)
+    vcp(A("ZB", 15, 143, 16), A("B", 0, 128, 16))
+    vcp(A("Z0", 15, 143, 16), A("G8"))
+    vcp(A("Z15", 15, 143, 16), A("G15"))
+    vts(A("Z8", 15, 143, 16), A("G8"), -8192.0, OP.mult)
+    vts(A("BB"), A("B"), 1048576.0, OP.mult)
+    vts(A("NI"), A("I"), -1.0, OP.mult)
+    vts(A("UN"), A("UP"), -1.0, OP.mult)
+    sel(A("W3"), A("UN"), [[-1, 128]], OP.not_equal, 1000.0, 0, 1)
+    for h in range(2):
+        vts(A("OH%d" % h), A("OT%d" % h), -2048.0, OP.add)
+    for h in range(2):
+        mm(A("P5", 128 * h, 128 * h + 128), A("OH%d" % h), A("I"))
+    vts(A("OLU"), A("P5", 0, 256), 2048.0, OP.add)
+    vts(A("CF"), A("CI"), -2048.0, OP.add)
+    collect(A("P7", 0, 64), "Z0", lambda x: A("CF", x, 1024, 16))
+    collect(A("P7", 64, 128), "Z15", lambda x: A("CF", x, 1024, 16))
+    vcp(A("CU", 0, 256), A("CI", 0, 256))
+    vts(A("LS"), A("P7", 0, 128), 2048.0, OP.add)
+    vms(A("SK", 4095, 4096), -14.0 / 1024)
+    for k in range(8):
+        o, i = A("WA", 512 + 512 * k, 1024 + 512 * k), ind(A("SK"), A("OLU", 32 * k, 32 * k + 32))
+        if k % 2 == 0:
+            vts(o, i, 1024.0, OP.mult, float(K0), OP.add)
+        else:
+            act(o, i, FN.Identity, float(K0), 1024.0)
+    vts(A("NN"), A("ND"), -1024.0, OP.mult)
+    vts(A("OCH"), A("OCN"), -2048.0, OP.add)
+
+    def number(k):
+        ps = "P6" if k % 2 == 0 else "P7"
+        for h in range(2):
+            x = 2 * k + h
+            mm(A(ps, 256 * h, 256 * h + 256), A("PX", 128 * x, 128 * x + 128), A("OCH"))
+        act(A("OO", 512 + 512 * k, 1024 + 512 * k), A(ps, 0, 512), FN.Silu, 2080.0)
+
+    def covers(t):
+        vts(A("CLF"), ind(A("COV"), A("LS", 16 * t, 16 * t + 16)), -2048.0, OP.add)
+        vts(A("CLU"), A("CLF"), 2048.0, OP.add)
+
+    def moved():
+        act(ind(A("OO"), A("OFS", 0, 16)), A("OV"), FN.Silu)
+
+    win = ["WA", "WB"]
+    for t in range(4):
+        W, N = win[t % 2], win[1 - t % 2]
+        wst, nst = A(W, 512, 4608), A(N, 512, 4608)
+        brep = []
+        for i in range(16):
+            brep.append((A("BRF", i, VL * 16, 16), A("BT", 0, VL), VL))
+            brep.append((A("BRH", i, 4096 - VL * 16, 16), A("BS", VL, 256), 256 - VL))
+
+        def Dc(c, a, b, s=1):
+            return A("D%d" % c, a, b, s)
+
+        def own(k):
+            if k == 0:
+                act(A("BS", 256, 512), ind(wst, A("LS", 64 + 16 * t, 80 + 16 * t)), FN.Copy)
+                return
+            act(A("BS", 0, 256), ind(wst, A("LS", 16 * t, 16 * t + 16)), FN.Copy)
+            act(A("BT"), A("BS", 0, 256), FN.Identity, -float(TOL))
+
+        def gather(c, q):
+            l0, n = CH[c]
+            o, i = Dc(c, 1, 1 + 16 * n), ind(wst, A("CU", 256 * t + l0, 256 * t + l0 + n))
+            if q == "V":
+                vcp(o, i)
+            else:
+                act(o, i, FN.Copy)
+
+        def repeat(k):
+            for j in range(k):
+                o, i, m = brep.pop(0)
+                gcp(o, i, m)
+
+        def psum(c, a, b, s=1):
+            name, off = (("TA", 0), ("TA", 512), ("TB", 0), ("TA", 0), ("TB", 0))[c]
+            return A(name, off + a, off + b, s)
+
+        def scan(c):
+            l0, n = CH[c]
+            if c < 4:
+                vcp(Dc(c, 0, 16 * n, 16), A("NN", 192 * t + l0, 192 * t + l0 + n))
+            elif t:
+                ev = ("arr%d" % (t - 1), len(topo.engines(T.cores[rank - 1], core)))
+                record("net", ev, [], [A("AV%d" % (t - 1))])
+                vts(Dc(4, 0, 1024, 16), A("AV%d" % (t - 1)), -1024.0, OP.mult)
+                vts(A("NA"), A("AV%d" % (t - 1)), -1024.0, OP.mult)
+            else:
+                vms(Dc(4, 0, 1024, 16), 0.0)
+            r = A("R", 16 * l0, 16 * l0 + 16 * n) if c < 4 else A("RF")
+            scan_(r, A("DM", 0, 16 * n), Dc(c, 0, 16 * n), 0.0)
+            vts(A("IN1", 16 * l0, 16 * l0 + 16 * n), r, -512.0, OP.is_ge, -15.5 / 16, OP.add)
+            for k in range(n // 32):
+                mm(psum(c, 512 * k, 512 * k + 512), A("BB"), A("IN1", 16 * l0 + 512 * k, 16 * l0 + 512 * k + 512))
+
+        def total(c):
+            l0, n = CH[c]
+            if t < 3 and c < 3 or t < 3 and c == 3:
+                for p in range(16):
+                    mm(A("P4", l0, l0 + n), A("I"), Dc(c, p, 16 * n, 16), p == 0, False)
+                mm(A("P4", l0, l0 + n), A("I"), A("BS", 256 + l0, 256 + l0 + n), False, True)
+
+        def leave(c):
+            l0, n = CH[c]
+            vtt(A("X", 16 * l0, 16 * l0 + 16 * n), Dc(c, 1, 1 + 16 * n), psum(c, 0, 16 * n), OP.min)
+            vtt(A("X", 16 * l0 + 15, 16 * l0 + 16 * n, 16), A("BS", 256 + l0, 256 + l0 + n), psum(c, 15, 16 * n, 16), OP.min)
+            act(ind(nst, A("CU", 256 * t + l0, 256 * t + l0 + n)), A("X", 16 * l0, 16 * l0 + 16 * n), FN.Silu)
+
+        def lost(k):
+            if k == 0:
+                collect(A("P5", 256, 268), "ZB", lambda x: A("NN", 192 * t + x, 192 * t + 192, 16))
+                collect(A("P5", 272, 288), "ZB", lambda x: A("BS", x, 256, 16))
+            else:
+                collect(A("P5", 268, 272), "ZB", lambda x: A("NA", x, 64, 16))
+
+        def numbers(c):
+            if t == 0:
+                for j in range(c):
+                    number(nn[0])
+                    nn[0] += 1
+
+        do = {"v": lambda c: gather(c, "V"), "a": lambda c: gather(c, "S"), "b": own, "r": repeat, "s": scan, "t": total, "l": leave, "q": lost, "n": numbers}
+        for step in STEP1.split():
+            do[step[0]](int(step[1:]))
+        if t == 0:
+            covers(0)
+            vcp(A("CU", 256, 1024), A("CI", 256, 1024))
+            vts(A("KS"), A("LS", 0, 64), 512.0, OP.add)
+        if t < 3:
+            vtt(A("AR"), A("RF", 15, 1024, 16), A("BS", 448, 512), OP.add)
+            vts(A("RR", 0, 192), A("P4", 0, 192), -1.0 / 1024, OP.mult, 0.0, OP.max)
+            vts(A("RR", 192, 256), A("AR"), -1.0 / 1024, OP.mult, 0.0, OP.max)
+            vts(A("U01"), A("RR"), 0.5, OP.is_gt)
+
+        def unmet(c):
+            if t < 3:
+                collect(A("P5", 0, 16), "ZB", lambda x: A("U01", x, 256, 16))
+
+        def lost2(c):
+            vts(A("L1"), A("P5", 256, 272), -512.0, OP.is_lt)
+            vts(A("L2"), A("P5", 272, 288), float(TOL), OP.is_ge)
+            vtt(A("LOST"), A("L1"), A("L2"), OP.mult)
+
+        def slots(c):
+            if t < 3:
+                vts(A("UL"), A("P5", 0, 16), 0.5, OP.is_ge)
+                vts(A("UK"), A("P5", 0, 16), 0.5, OP.is_lt)
+                mm(A("P5", 16, 32), A("B"), A("UL"))
+                mm(A("P5", 32, 48), A("W3"), A("UL"))
+
+        def slots2(c):
+            if t < 3:
+                vtt(A("UK2"), A("UK"), A("KM"), OP.mult)
+                scan_(A("CY"), A("ON16"), A("P5", 16, 32), -1001.0)
+                vtt(A("SP"), A("P5", 32, 48), A("CY"), OP.add)
+                vtt(A("OF"), A("SP"), A("UK2"), OP.max)
+                vcp(A("OU"), A("OF"))
+
+        def spsum(k):
+            return A(*(("TA", 0, 512), ("TA", 512, 1024), ("TB", 0, 512))[k])
+
+        def sgather(k):
+            l0, n = SG3[k]
+            ga, br = A("GA", 16 * (l0 - VL), 16 * (l0 - VL + n)), A("BRH", 16 * (l0 - VL), 16 * (l0 - VL + n))
+            act(ga, ind(nst, A("CLU", l0, l0 + n)), FN.Copy)
+            mm(spsum(k), A("NI"), br, True, False)
+            mm(spsum(k), A("I"), ga, False, True)
+
+        def ssign(k):
+            l0, n = SG3[k]
+            act(A("SGN", 16 * (l0 - VL), 16 * (l0 - VL + n)), spsum(k), FN.Sign, float(TOL))
+
+        def fused(k):
+            l0, n = FG[k]
+            vtt(A("IN3", 16 * l0, 16 * (l0 + n)), ind(nst, A("CLU", l0, l0 + n)), A("BRF", 16 * l0, 16 * (l0 + n)), OP.is_ge)
+
+        def counts(k):
+            p, l0, n = PART[k]
+            for i in range(16):
+                r = A("IN3", 16 * l0 + i, 16 * (l0 + n), 16) if l0 < VL else A("SGN", 16 * (l0 - VL) + i, 16 * (l0 - VL + n), 16)
+                mm(A(p, 0, n), EX("ZB", i), r, i == 0, i == 15)
+
+        def fits(k):
+            p, l0, n = PART[k]
+            vts(A("F", l0, l0 + n), A(p, 0, n), 8.5 if l0 < VL else 1.0, OP.is_ge)
+            mm(A(p, 256, 256 + n), A("TRI"), A("F", l0, l0 + n))
+
+        def first(k):
+            p, l0, n = PART[k]
+            vtt(A("SM", 256 + l0, 256 + l0 + n), A("F", l0, l0 + n), A(p, 256, 256 + n), OP.is_gt)
+            vtt(A("SM", l0, l0 + n), A("SM", 256 + l0, 256 + l0 + n), A("CLF", l0, l0 + n), OP.mult)
+
+        def moved_before(c):
+            if t:
+                moved()
+
+        do = {"u": unmet, "g": sgather, "s": ssign, "v": fused, "c": counts, "f": fits, "o": first, "L": lost2, "p": slots, "P": slots2, "m": moved_before}
+        for step in STEP3.split():
+            do[step[0]](int(step[1:]))
+        mm(A("P4", 0, 256), A("B"), A("SM", 0, 256))
+        collect(A("P5", 64, 96), "ZB", lambda x: A("SM", x, 512, 16))
+        act(A("CR"), A("P4", 0, 256), FN.Copy)
+        if t < 3:
+            covers(t + 1)
+        vcp(A("CLI"), A("P5", 64, 80))
+        vtt(A("OKL"), A("P5", 80, 96), A("LOST"), OP.mult)
+        vts(A("MLU"), A("P5", 64, 80), 2048.0, OP.add)
+        act(A("VB", 0, 256), ind(nst, A("MLU")), FN.Copy)
+        act(A("OV"), ind(A("OO", 512, 4608), A("MLU")), FN.Copy)
+        mm(A("P4", 0, 256), A("B"), A("ZZ"), True, False)
+        for y in range(16):
+            ey = (T.E[:, y, 0:256 - 16 * y], [("E", 256 * y, 256 * y + 256)])
+            vts(ey, A("CR", 16 * y, 256), A("CLI", y, y + 1), OP.is_equal, A("OKL", y, y + 1), OP.mult)
+            if y < 15:
+                mm(A("P4", 16 * y + 16, 256), A("B"), (T.E[:, y, 16:256 - 16 * y], ey[1]), False, False)
+        md = (T.MD[:, :, :], [("MD", 0, 16)])
+        vtt(md, (T.E[:, :, 0:16], [("E", 0, 4096)]), mk, OP.mult)
+        mm(A("P4", 0, 256), A("B"), md, False, True)
+        vts(A("OB"), A("OKL"), 8192.0, OP.mult, -8192.0, OP.add)
+        vts(A("CLM"), A("CLI"), 2560.0, OP.add)
+        vtt(A("R2", 0, 16), A("OB"), A("KS", 16 * t, 16 * t + 16), OP.add)
+        vtt(A("R2", 16, 32), A("OB"), A("CLM"), OP.add)
+        vcp(A("DL"), A("P4", 0, 256))
+        collect(A("P5", 128, 144), "Z8", lambda x: A("DL", x, 256, 16))
+        if t < 3:
+            vcp(ind(A("SW%d" % t), A("OU")), A("RR"))
+            dst = T.cores[(rank + 1) % len(T.cores)]
+            addr = topo.addr(dst)
+            src = A("SW%d" % t, 0, 64)
+            waits("G", [src], [])
+            g.remote_dma(out_ap=T["AV%d" % t][:, :], in_ap=src[0], remote_sem=T.sem["arr%d" % t], local_sem=T.sem["loc%d" % t],
+                         pid=addr[1], routing_id=addr[0], dma_engine_mask=topo.mask(core, dst))
+        vtt(A("R3", 0, 16), A("P5", 128, 144), A("R2", 0, 16), OP.add)
+        vtt(A("R3", 16, 32), A("P5", 128, 144), A("R2", 16, 32), OP.add)
+        vtt(A("R4"), A("R3"), A("KD"), OP.max)
+        vcp(A("OFS"), A("R4"))
+        vcp(ind(A(N), A("OFS")), A("VB"))
+    moved()
+    dma("Y", T.ZF[:, :], T.WA[0:128:16, 512:4608], [A("WA", 512, 4608)], [A("ZF")])
+    dma("Y", T.OFN[:, :], T.OO[0:128:16, 512:4608], [A("OO", 512, 4608)], [A("OFN")])
+    vts(A("EF"), A("ZF"), float(TOL), OP.is_lt, 4095.0, OP.mult)
+    vts(A("OI"), A("OFN"), -32.0, OP.add)
+    vtt(A("YF"), A("OI"), A("EF"), OP.max)
+    need_event("Y", dma("Y", T.y[:, :], T.YF[:, :], [A("YF")], []))
+    for t in range(3):
+        g.wait_ge(T.sem["loc%d" % t], len(topo.engines(core, T.cores[(rank + 1) % len(T.cores)])))
+    for s in ("cV", "cS", "cT", "cG"):
+        need_event("G", (s, count[s]))

@@ -4,23 +4,22 @@ OP = AluOpType
 FN = ActivationFunctionType
 K0, TOL = 14, 7
 CH = [(0, 32), (32, 32), (64, 64), (128, 64), (192, 64)]
-VL = 160
-FG = [(0, 64), (64, 64), (128, 32)]
-SG3 = [(160, 32), (192, 32), (224, 32)]
-PART = [("P6", 0, 64), ("P7", 64, 64), ("P6", 128, 32), ("P4", 160, 96)]
-STEP1 = "v0 a1 b0 a2 b1 n3 s0 s1 l0 l1 n2 r32 t0 t1 s2 v3 l2 q0 n3 s3 t2 v4 l3 s4 q1 t3 l4"
-STEP3 = "u0 g0 g1 v0 c0 s0 g2 v1 f0 o0 c1 s1 s2 m0 v2 c3 f1 o1 c2 L0 p0 f3 o3 P0 f2 o2"
+VL = 176
+FG = [(0, 64), (64, 64), (128, 48)]
+SG3 = [(176, 32), (208, 32), (240, 16)]
+PART = [("P6", 0, 128), ("P4", 128, 128)]
+STEP1 = "v0 a1 b0 a2 b1 s0+s1 l0+l1+s2 r32 t0 t1 v3 l2+s3 q0 t2 v4 l3 t3 s4 q1 x0+y0 l4"
+STEP3 = "u0 L0+p0 P0 Q0 g0 g1 v0 c0 s0 g2 v1 s1 c3 c2 s2 m0 v2 f0 c1 c4 o0+C0 f1 o1"
 
 _sb = {
-    "OT0": (128, "int32"), "OT1": (128, "int32"), "OH0": (128, "float16"), "OH1": (128, "float16"), "OLU": (256, "uint16"),
-    "OCN": (256, "int32"), "OCH": (256, "float16"),
+    "OH": (4096, "float16"), "OLU": (256, "uint16"), "OCN": (256, "int32"), "OCH": (256, "float16"),
     "SK": (4096, "bfloat16"), "COV": (4096, "int32"), "CI": (1024, "int32"), "CU": (1024, "uint16"), "CF": (1024, "float16"),
     "ND": (768, "bfloat16"), "NN": (768, "bfloat16"), "LS": (128, "uint16"), "KS": (64, "float32"),
     "WA": (4608, "float32"), "WB": (4608, "float32"), "OO": (4608, "float32"),
-    "ONE": (2048, "bfloat16"), "I": (128, "bfloat16"), "NI": (128, "bfloat16"), "B": (128, "bfloat16"), "BB": (128, "bfloat16"),
-    "PX": (2048, "bfloat16"), "ZB": (144, "bfloat16"), "Z0": (144, "bfloat16"), "Z15": (144, "bfloat16"), "Z8": (144, "bfloat16"),
-    "G8": (8, "bfloat16"), "G15": (8, "bfloat16"),
-    "TRI": (128, "bfloat16"), "UP": (128, "bfloat16"), "UN": (128, "bfloat16"), "W3": (128, "bfloat16"),
+    "ONE": (512, "bfloat16"), "I": (128, "bfloat16"), "NI": (128, "bfloat16"), "B": (128, "bfloat16"), "BB": (128, "bfloat16"),
+    "PX": (2048, "bfloat16"), "ZB": (144, "bfloat16"), "ZH": (144, "bfloat16"), "CM": (128, "bfloat16"),
+    "Z0": (144, "bfloat16"), "Z15": (144, "bfloat16"), "Z8": (144, "bfloat16"), "G8": (8, "bfloat16"), "G15": (8, "bfloat16"),
+    "TRI": (128, "bfloat16"), "UP": (128, "bfloat16"), "UN": (128, "bfloat16"), "UM": (128, "bfloat16"), "W3": (128, "bfloat16"),
     "PI": (1, "int32"), "PA": (1, "int32"), "XC": (1, "float32"), "ZR": (256, "float32"), "LY": (16, "float32"), "KM": (16, "float32"),
     "KD": (32, "float32"), "DM": (1024, "bfloat16"), "ON16": (16, "float32"), "ZZ": (256, "bfloat16"),
     "D0": (528, "bfloat16"), "D1": (528, "bfloat16"), "D2": (1040, "bfloat16"), "D3": (1040, "bfloat16"), "D4": (1040, "float32"),
@@ -28,9 +27,10 @@ _sb = {
     "NA": (64, "bfloat16"), "AR": (64, "float32"), "RR": (256, "float32"), "U01": (256, "bfloat16"), "UL": (16, "bfloat16"),
     "UK": (16, "float32"), "UK2": (16, "float32"), "CY": (16, "float32"), "SP": (16, "float32"), "OF": (16, "float32"), "OU": (16, "uint16"),
     "BS": (512, "bfloat16"), "BT": (256, "float32"), "BRF": (VL * 16, "float32"), "BRH": (4096 - VL * 16, "bfloat16"),
-    "CLF": (256, "float16"), "CLU": (256, "uint16"), "IN3": (VL * 16, "bfloat16"), "GA": (4096 - VL * 16, "bfloat16"), "SGN": (4096 - VL * 16, "bfloat16"),
+    "CLF0": (256, "float16"), "CLU0": (256, "uint16"), "CLF1": (256, "float16"), "CLU1": (256, "uint16"),
+    "IN3": (VL * 16, "bfloat16"), "GA": (4096 - VL * 16, "bfloat16"), "SGN": (4096 - VL * 16, "bfloat16"),
     "L1": (16, "float32"), "L2": (16, "float32"), "LOST": (16, "float32"),
-    "F": (256, "bfloat16"), "SM": (512, "float16"), "CR": (256, "float16"), "CLI": (16, "float32"), "OKL": (16, "float32"), "OB": (16, "float32"),
+    "F": (256, "bfloat16"), "SM": (512, "float16"), "CR": (256, "float16"), "OKL": (16, "float32"), "OB": (16, "float32"),
     "CLM": (16, "float32"), "R2": (32, "float32"), "R3": (32, "float32"), "R4": (32, "float32"), "OFS": (32, "uint16"), "MLU": (16, "uint16"),
     "VB": (512, "float32"), "OV": (256, "float32"),
     "DL": (256, "bfloat16"), "ZF": (256, "float32"), "OFN": (256, "float32"), "OI": (256, "int32"), "EF": (256, "float32"), "YF": (256, "float32"),
@@ -47,7 +47,7 @@ SCRATCH["TB"] = ("psum", [128, 1024], "float32")
 for _t in range(4, 8):
     SCRATCH["P%d" % _t] = ("psum", [128, 512], "float32")
 PS = ("TA", "TB", "P4", "P5", "P6", "P7")
-SEMAPHORES = ["cV", "cS", "cT", "cG"] + ["arr%d" % t for t in range(3)] + ["loc%d" % t for t in range(3)] + ["d%d" % k for k in range(24)]
+SEMAPHORES = ["cV", "cS", "cT", "cG"] + ["arr%d" % t for t in range(3)] + ["loc%d" % t for t in range(3)] + ["d%d" % k for k in range(8)]
 
 
 def rank_program(g, core, T, topo):
@@ -59,7 +59,8 @@ def rank_program(g, core, T, topo):
     known = {q: {} for q in queues}
     clocks = {}
     log = {}
-    nd, nn = [0], [0]
+    nd = [0]
+    hold = [None]
 
     def A(name, a=0, b=None, s=1):
         n = SCRATCH[name][1][1]
@@ -121,6 +122,9 @@ def rank_program(g, core, T, topo):
             need_event(q, (s, v))
 
     def emit(q, fn, reads, writes):
+        if hold[0] is not None:
+            hold[0].append((q, fn, reads, writes))
+            return
         waits(q, reads, writes)
         sem = "c" + q
         inst = fn()
@@ -129,6 +133,26 @@ def rank_program(g, core, T, topo):
         ev = (sem, count[sem])
         clocks[ev] = dict(known[q])
         record(q, ev, reads, writes)
+
+    def together(parts):
+        if len(parts) == 1:
+            return parts[0]()
+        lists = []
+        for f in parts:
+            hold[0] = []
+            f()
+            units = []
+            for call in hold[0]:
+                if call[0] == "V" or not units:
+                    units.append([])
+                units[-1].append(call)
+            lists.append(units)
+        hold[0] = None
+        while any(lists):
+            for units in lists:
+                if units:
+                    for call in units.pop(0):
+                        emit(*call)
 
     def dma(q, out, in_, reads, writes):
         waits(q, reads, writes)
@@ -190,64 +214,73 @@ def rank_program(g, core, T, topo):
         for x in range(16):
             mm(out, EX(name, x), rhs(x), x == 0, x == 15)
 
-    for h in range(2):
-        for d in range(8):
-            o = A("OT%d" % h, 16 * d, 16 * d + 16)
-            dma("Y" if h == 0 else "S", o[0], T.occ[d, 2048 * h:2048 * h + 2048], [], [o])
-    dma("S", T.SK[:, :], T.skill[:, :], [], [A("SK")])
-    dma("Y", T.CI[:, :], T.cards[:, :], [], [A("CI")])
+    dma("S", T.OCN[:, :], T.occ[:, :], [], [A("OCN")])
+    dma("S", T.CI[:, :], T.cards[:, :], [], [A("CI")])
+    skills = dma("S", T.SK[:, :], T.skill[:, :], [], [A("SK")])
     dma("Y", T.ND[:, :], T.need[:, :], [], [A("ND")])
-    dma("Y", T.OCN[:, :], T.occ[:, :], [], [A("OCN")])
+    need_event("Y", skills)
     dma("Y", T.COV[:, :], T.cover[:, :], [], [A("COV")])
 
     iota(A("PI"), [[0, 1]], 0, 1, False)
-    iota(A("ZR"), [[0, 16], [1, 16]], 0, 0)
-    iota(A("LY"), [[16, 16]], 0, 0)
     vms(A("ONE"), 1.0)
-    for z in ("ZB", "Z0", "Z8", "Z15"):
+    for z in ("Z0", "ZB", "Z8", "Z15"):
         vms(A(z), 0.0)
-    vms(A("DM"), 1.0)
-    vms(A("DM", 0, 1024, 16), 0.0)
+    vms(A("CM"), -1.0 / 16)
+    sel(A("G8"), A("ONE", 0, 8), [[-16, 8]], OP.is_equal, 0.0, 0, 1)
+    iota(A("ZR"), [[0, 16], [1, 16]], 0, 0)
+    for k in range(4):
+        sel(A("PX", 512 * k, 512 * k + 512), A("ONE"), [[-1, 4], [-16, 8], [0, 16]], OP.is_equal, 0.0, -4 * k, 1)
+    iota(A("LY"), [[16, 16]], 0, 0)
+    sel(A("G15"), A("ONE", 0, 8), [[-16, 8]], OP.is_equal, 0.0, -15, 1)
     sel(A("I"), A("ONE", 0, 128), [[-1, 128]], OP.is_equal, 0.0, 0, 1)
     sel(A("UN"), A("ONE", 0, 128), [[-16, 8], [0, 16]], OP.is_ge, 0.0, 0, 1)
     sel(A("B"), A("UN"), [[16, 8], [0, 16]], OP.is_ge, 0.0, 15, -1)
-    sel(A("G8"), A("ONE", 0, 8), [[-16, 8]], OP.is_equal, 0.0, 0, 1)
-    sel(A("G15"), A("ONE", 0, 8), [[-16, 8]], OP.is_equal, 0.0, -15, 1)
-    sel(A("TRI"), A("B"), [[1, 128]], OP.is_gt, 0.0, 0, -1)
     sel(A("UP"), A("B"), [[-1, 128]], OP.is_gt, 0.0, 0, 1)
-    sel(A("PX"), A("ONE"), [[-1, 16], [-16, 8], [0, 16]], OP.is_equal, 0.0, 0, 1)
+    for h in range(2):
+        sel(A("DM", 512 * h, 512 * h + 512), A("ONE"), [[0, 32], [1, 16]], OP.is_gt, 0.0, 0, 0)
+    sel(A("TRI"), A("B"), [[1, 128]], OP.is_gt, 0.0, 0, -1)
+    iota(A("VB", 256, 512), [[0, 256]], 0, 0)
+    iota(A("ON16"), [[0, 16]], 1, 0)
+    iota(A("ZZ"), [[0, 256]], 0, 0)
+    iota(A("NA"), [[0, 64]], 0, 0)
     for t in range(3):
         iota(A("SW%d" % t, 0, 64), [[0, 64]], 0, 0, False)
-    vms(A("VB", 256, 512), 0.0)
-    vms(A("ON16"), 1.0)
-    vms(A("ZZ"), 0.0)
-    vms(A("NA"), 0.0)
+    vcp(A("Z0", 15, 143, 16), A("G8"))
+    vts(A("Z8", 15, 143, 16), A("G8"), -8192.0, OP.mult)
     vts(A("PA"), A("PI"), 15, OP.bitwise_and)
     vcp(A("XC"), A("PA"))
     mk = (T.MK[:, :, :], [("MK", 0, 16)])
     for y in range(16):
         vts((T.MK[:, y, :], [("MK", y, y + 1)]), A("ZR", 0, 16), A("XC"), OP.is_gt)
+    vts(A("OCH"), A("OCN"), -2048.0, OP.add)
+    for k in range(8):
+        ps, c = (("P6", 0), ("P7", 0), ("TA", 0), ("TA", 512), ("TB", 0), ("TB", 512), ("P4", 0), ("P6", 0))[k]
+        for h in range(2):
+            x = 2 * k + h
+            mm(A(ps, c + 256 * h, c + 256 * h + 256), A("PX", 128 * x, 128 * x + 128), A("OCH"))
+        if k % 2 == 0:
+            vcp(A("OH", 512 * k, 512 * k + 512), A(ps, c, c + 512))
+        else:
+            act(A("OH", 512 * k, 512 * k + 512), A(ps, c, c + 512), FN.Copy)
+    collect(A("P5", 0, 256), "Z0", lambda x: A("OH", x, 4096, 16))
+    vts(A("CF"), A("CI"), -2048.0, OP.add)
+    vcp(A("Z15", 15, 143, 16), A("G15"))
+    collect(A("P7", 0, 64), "Z0", lambda x: A("CF", x, 1024, 16))
+    collect(A("P7", 64, 128), "Z15", lambda x: A("CF", x, 1024, 16))
+    vcp(A("CU"), A("CI"))
+    vts(A("OLU"), A("P5", 0, 256), 2048.0, OP.add)
     vts(A("KD", 0, 16), A("LY"), A("XC"), OP.add)
     vts(A("KD", 16, 32), A("KD", 0, 16), 256.0, OP.add)
     vts(A("KM"), A("KD", 0, 16), 256.0, OP.add)
     vcp(A("ZB", 15, 143, 16), A("B", 0, 128, 16))
-    vcp(A("Z0", 15, 143, 16), A("G8"))
-    vcp(A("Z15", 15, 143, 16), A("G15"))
-    vts(A("Z8", 15, 143, 16), A("G8"), -8192.0, OP.mult)
     vts(A("BB"), A("B"), 1048576.0, OP.mult)
+    vts(A("ZH"), A("ZB"), 0.5, OP.mult)
     vts(A("NI"), A("I"), -1.0, OP.mult)
-    vts(A("UN"), A("UP"), -1.0, OP.mult)
-    sel(A("W3"), A("UN"), [[-1, 128]], OP.not_equal, 1000.0, 0, 1)
-    for h in range(2):
-        vts(A("OH%d" % h), A("OT%d" % h), -2048.0, OP.add)
-    for h in range(2):
-        mm(A("P5", 128 * h, 128 * h + 128), A("OH%d" % h), A("I"))
-    vts(A("OLU"), A("P5", 0, 256), 2048.0, OP.add)
-    vts(A("CF"), A("CI"), -2048.0, OP.add)
-    collect(A("P7", 0, 64), "Z0", lambda x: A("CF", x, 1024, 16))
-    collect(A("P7", 64, 128), "Z15", lambda x: A("CF", x, 1024, 16))
-    vcp(A("CU", 0, 256), A("CI", 0, 256))
+    vts(A("UM"), A("UP"), -1.0, OP.mult)
+    sel(A("W3"), A("UM"), [[-1, 128]], OP.not_equal, 1000.0, 0, 1)
     vts(A("LS"), A("P7", 0, 128), 2048.0, OP.add)
+    vts(A("KS"), A("LS", 0, 64), 512.0, OP.add)
+    vts(A("NN"), A("ND"), -1024.0, OP.mult)
     vms(A("SK", 4095, 4096), -14.0 / 1024)
     for k in range(8):
         o, i = A("WA", 512 + 512 * k, 1024 + 512 * k), ind(A("SK"), A("OLU", 32 * k, 32 * k + 32))
@@ -255,19 +288,11 @@ def rank_program(g, core, T, topo):
             vts(o, i, 1024.0, OP.mult, float(K0), OP.add)
         else:
             act(o, i, FN.Identity, float(K0), 1024.0)
-    vts(A("NN"), A("ND"), -1024.0, OP.mult)
-    vts(A("OCH"), A("OCN"), -2048.0, OP.add)
-
-    def number(k):
-        ps = "P6" if k % 2 == 0 else "P7"
-        for h in range(2):
-            x = 2 * k + h
-            mm(A(ps, 256 * h, 256 * h + 256), A("PX", 128 * x, 128 * x + 128), A("OCH"))
-        act(A("OO", 512 + 512 * k, 1024 + 512 * k), A(ps, 0, 512), FN.Silu, 2080.0)
 
     def covers(t):
-        vts(A("CLF"), ind(A("COV"), A("LS", 16 * t, 16 * t + 16)), -2048.0, OP.add)
-        vts(A("CLU"), A("CLF"), 2048.0, OP.add)
+        f, u = "CLF%d" % (t % 2), "CLU%d" % (t % 2)
+        vts(A(f), ind(A("COV"), A("LS", 16 * t, 16 * t + 16)), -2048.0, OP.add)
+        vts(A(u), A(f), 2048.0, OP.add)
 
     def moved():
         act(ind(A("OO"), A("OFS", 0, 16)), A("OV"), FN.Silu)
@@ -276,10 +301,9 @@ def rank_program(g, core, T, topo):
     for t in range(4):
         W, N = win[t % 2], win[1 - t % 2]
         wst, nst = A(W, 512, 4608), A(N, 512, 4608)
-        brep = []
-        for i in range(16):
-            brep.append((A("BRF", i, VL * 16, 16), A("BT", 0, VL), VL))
-            brep.append((A("BRH", i, 4096 - VL * 16, 16), A("BS", VL, 256), 256 - VL))
+        clf, clu = "CLF%d" % (t % 2), "CLU%d" % (t % 2)
+        brep = [(A("BRF", i, VL * 16, 16), A("BT", 0, VL), VL) for i in range(16)]
+        brep += [(A("BRH", i, 4096 - VL * 16, 16), A("BS", VL, 256), 256 - VL) for i in range(16)]
 
         def Dc(c, a, b, s=1):
             return A("D%d" % c, a, b, s)
@@ -327,7 +351,7 @@ def rank_program(g, core, T, topo):
 
         def total(c):
             l0, n = CH[c]
-            if t < 3 and c < 3 or t < 3 and c == 3:
+            if t < 3:
                 for p in range(16):
                     mm(A("P4", l0, l0 + n), A("I"), Dc(c, p, 16 * n, 16), p == 0, False)
                 mm(A("P4", l0, l0 + n), A("I"), A("BS", 256 + l0, 256 + l0 + n), False, True)
@@ -345,24 +369,24 @@ def rank_program(g, core, T, topo):
             else:
                 collect(A("P5", 268, 272), "ZB", lambda x: A("NA", x, 64, 16))
 
-        def numbers(c):
-            if t == 0:
-                for j in range(c):
-                    number(nn[0])
-                    nn[0] += 1
+        def rest(c):
+            if t < 3:
+                vtt(A("AR"), A("RF", 15, 1024, 16), A("BS", 448, 512), OP.add)
+                vts(A("RR", 192, 256), A("AR"), -1.0 / 1024, OP.mult, 0.0, OP.max)
 
-        do = {"v": lambda c: gather(c, "V"), "a": lambda c: gather(c, "S"), "b": own, "r": repeat, "s": scan, "t": total, "l": leave, "q": lost, "n": numbers}
-        for step in STEP1.split():
-            do[step[0]](int(step[1:]))
+        def rest2(c):
+            if t < 3:
+                vts(A("RR", 0, 192), A("P4", 0, 192), -1.0 / 1024, OP.mult, 0.0, OP.max)
+                vts(A("U01"), A("RR"), 0.5, OP.is_gt)
+
+        def run(order, do):
+            for step in order.split():
+                together([(lambda s=s: do[s[0]](int(s[1:]))) for s in step.split("+")])
+
+        run(STEP1, {"v": lambda c: gather(c, "V"), "a": lambda c: gather(c, "S"), "b": own, "r": repeat, "s": scan, "t": total,
+                    "l": leave, "q": lost, "x": rest, "y": rest2})
         if t == 0:
             covers(0)
-            vcp(A("CU", 256, 1024), A("CI", 256, 1024))
-            vts(A("KS"), A("LS", 0, 64), 512.0, OP.add)
-        if t < 3:
-            vtt(A("AR"), A("RF", 15, 1024, 16), A("BS", 448, 512), OP.add)
-            vts(A("RR", 0, 192), A("P4", 0, 192), -1.0 / 1024, OP.mult, 0.0, OP.max)
-            vts(A("RR", 192, 256), A("AR"), -1.0 / 1024, OP.mult, 0.0, OP.max)
-            vts(A("U01"), A("RR"), 0.5, OP.is_gt)
 
         def unmet(c):
             if t < 3:
@@ -388,13 +412,17 @@ def rank_program(g, core, T, topo):
                 vtt(A("OF"), A("SP"), A("UK2"), OP.max)
                 vcp(A("OU"), A("OF"))
 
+        def slots3(c):
+            if t < 3:
+                vcp(ind(A("SW%d" % t), A("OU")), A("RR"))
+
         def spsum(k):
-            return A(*(("TA", 0, 512), ("TA", 512, 1024), ("TB", 0, 512))[k])
+            return A(*(("TA", 0, 512), ("TA", 512, 1024), ("TB", 0, 16 * SG3[2][1]))[k])
 
         def sgather(k):
             l0, n = SG3[k]
             ga, br = A("GA", 16 * (l0 - VL), 16 * (l0 - VL + n)), A("BRH", 16 * (l0 - VL), 16 * (l0 - VL + n))
-            act(ga, ind(nst, A("CLU", l0, l0 + n)), FN.Copy)
+            act(ga, ind(nst, A(clu, l0, l0 + n)), FN.Copy)
             mm(spsum(k), A("NI"), br, True, False)
             mm(spsum(k), A("I"), ga, False, True)
 
@@ -404,58 +432,66 @@ def rank_program(g, core, T, topo):
 
         def fused(k):
             l0, n = FG[k]
-            vtt(A("IN3", 16 * l0, 16 * (l0 + n)), ind(nst, A("CLU", l0, l0 + n)), A("BRF", 16 * l0, 16 * (l0 + n)), OP.is_ge)
+            vtt(A("IN3", 16 * l0, 16 * (l0 + n)), ind(nst, A(clu, l0, l0 + n)), A("BRF", 16 * l0, 16 * (l0 + n)), OP.is_ge)
 
         def counts(k):
-            p, l0, n = PART[k]
             for i in range(16):
-                r = A("IN3", 16 * l0 + i, 16 * (l0 + n), 16) if l0 < VL else A("SGN", 16 * (l0 - VL) + i, 16 * (l0 - VL + n), 16)
-                mm(A(p, 0, n), EX("ZB", i), r, i == 0, i == 15)
+                if k == 0 or k == 3:
+                    h = 64 if k else 0
+                    mm(A("P6", h, h + 64), EX("ZB", i), A("IN3", 16 * h + i, 16 * h + 1024, 16), i == 0, i == 15)
+                elif k == 1:
+                    mm(A("P4", 0, VL - 128), EX("ZB", i), A("IN3", 2048 + i, VL * 16, 16), i == 0, False)
+                else:
+                    a, b = ((0, 64), (64, 256 - VL))[k == 4]
+                    mm(A("P4", VL - 128 + a, VL - 128 + b), EX("ZH", i), A("SGN", 16 * a + i, 16 * b, 16), i == 0, i == 15)
+            if k == 1:
+                mm(A("P4", 0, VL - 128), A("CM"), A("ONE", 0, VL - 128), False, True)
 
         def fits(k):
             p, l0, n = PART[k]
-            vts(A("F", l0, l0 + n), A(p, 0, n), 8.5 if l0 < VL else 1.0, OP.is_ge)
+            vts(A("F", l0, l0 + n), A(p, 0, n), (8.5, 0.5)[k], OP.is_ge)
             mm(A(p, 256, 256 + n), A("TRI"), A("F", l0, l0 + n))
 
         def first(k):
             p, l0, n = PART[k]
             vtt(A("SM", 256 + l0, 256 + l0 + n), A("F", l0, l0 + n), A(p, 256, 256 + n), OP.is_gt)
-            vtt(A("SM", l0, l0 + n), A("SM", 256 + l0, 256 + l0 + n), A("CLF", l0, l0 + n), OP.mult)
+            vtt(A("SM", l0, l0 + n), A("SM", 256 + l0, 256 + l0 + n), A(clf, l0, l0 + n), OP.mult)
+
+        def covers_next(c):
+            if t < 3:
+                covers(t + 1)
 
         def moved_before(c):
             if t:
                 moved()
 
-        do = {"u": unmet, "g": sgather, "s": ssign, "v": fused, "c": counts, "f": fits, "o": first, "L": lost2, "p": slots, "P": slots2, "m": moved_before}
-        for step in STEP3.split():
-            do[step[0]](int(step[1:]))
+        run(STEP3, {"u": unmet, "g": sgather, "s": ssign, "v": fused, "c": counts, "f": fits, "o": first, "L": lost2, "p": slots,
+                    "P": slots2, "Q": slots3, "m": moved_before, "C": covers_next})
         mm(A("P4", 0, 256), A("B"), A("SM", 0, 256))
         collect(A("P5", 64, 96), "ZB", lambda x: A("SM", x, 512, 16))
         act(A("CR"), A("P4", 0, 256), FN.Copy)
-        if t < 3:
-            covers(t + 1)
-        vcp(A("CLI"), A("P5", 64, 80))
         vtt(A("OKL"), A("P5", 80, 96), A("LOST"), OP.mult)
         vts(A("MLU"), A("P5", 64, 80), 2048.0, OP.add)
         act(A("VB", 0, 256), ind(nst, A("MLU")), FN.Copy)
+        if t == 0:
+            act(A("OO", 512, 4608), A("OH"), FN.Silu, 2080.0)
         act(A("OV"), ind(A("OO", 512, 4608), A("MLU")), FN.Copy)
         mm(A("P4", 0, 256), A("B"), A("ZZ"), True, False)
         for y in range(16):
             ey = (T.E[:, y, 0:256 - 16 * y], [("E", 256 * y, 256 * y + 256)])
-            vts(ey, A("CR", 16 * y, 256), A("CLI", y, y + 1), OP.is_equal, A("OKL", y, y + 1), OP.mult)
+            vts(ey, A("CR", 16 * y, 256), A("P5", 64 + y, 65 + y), OP.is_equal, A("OKL", y, y + 1), OP.mult)
             if y < 15:
                 mm(A("P4", 16 * y + 16, 256), A("B"), (T.E[:, y, 16:256 - 16 * y], ey[1]), False, False)
         md = (T.MD[:, :, :], [("MD", 0, 16)])
         vtt(md, (T.E[:, :, 0:16], [("E", 0, 4096)]), mk, OP.mult)
         mm(A("P4", 0, 256), A("B"), md, False, True)
         vts(A("OB"), A("OKL"), 8192.0, OP.mult, -8192.0, OP.add)
-        vts(A("CLM"), A("CLI"), 2560.0, OP.add)
+        vts(A("CLM"), A("P5", 64, 80), 2560.0, OP.add)
         vtt(A("R2", 0, 16), A("OB"), A("KS", 16 * t, 16 * t + 16), OP.add)
         vtt(A("R2", 16, 32), A("OB"), A("CLM"), OP.add)
         vcp(A("DL"), A("P4", 0, 256))
         collect(A("P5", 128, 144), "Z8", lambda x: A("DL", x, 256, 16))
         if t < 3:
-            vcp(ind(A("SW%d" % t), A("OU")), A("RR"))
             dst = T.cores[(rank + 1) % len(T.cores)]
             addr = topo.addr(dst)
             src = A("SW%d" % t, 0, 64)

from concourse.mybir import AluOpType, ActivationFunctionType

OP = AluOpType
FN = ActivationFunctionType
K0, TOL = 14, 7
CH = [(0, 32), (32, 32), (64, 64), (128, 64), (192, 64)]
VL = 176
FG = [(0, 64), (64, 64), (128, 48)]
SG3 = [(176, 32), (208, 32), (240, 16)]
PART = [("P6", 0, 128), ("P4", 128, 128)]
STEP1 = "v0 a1 b0 a2 b1 s0+s1 l0+l1+s2 r32 t0 t1 v3 l2+s3 q0 t2 v4 l3 t3 s4 q1 x0+y0 l4"
STEP3 = "u0 L0+p0 P0 Q0 g0 g1 v0 c0 s0 g2 v1 s1 c3 c2 s2 m0 v2 f0 c1 c4 o0+C0 f1 o1"

_sb = {
    "OH": (4096, "float16"), "OLU": (256, "uint16"), "OCN": (256, "int32"), "OCH": (256, "float16"),
    "SK": (4096, "bfloat16"), "COV": (4096, "int32"), "CI": (1024, "int32"), "CU": (1024, "uint16"), "CF": (1024, "float16"),
    "ND": (768, "bfloat16"), "NN": (768, "bfloat16"), "LS": (128, "uint16"), "KS": (64, "float32"),
    "WA": (4608, "float32"), "WB": (4608, "float32"), "OO": (4608, "float32"),
    "ONE": (512, "bfloat16"), "I": (128, "bfloat16"), "NI": (128, "bfloat16"), "B": (128, "bfloat16"), "BB": (128, "bfloat16"),
    "PX": (2048, "bfloat16"), "ZB": (144, "bfloat16"), "ZH": (144, "bfloat16"), "CM": (128, "bfloat16"),
    "Z0": (144, "bfloat16"), "Z15": (144, "bfloat16"), "Z8": (144, "bfloat16"), "G8": (8, "bfloat16"), "G15": (8, "bfloat16"),
    "TRI": (128, "bfloat16"), "UP": (128, "bfloat16"), "UN": (128, "bfloat16"), "UM": (128, "bfloat16"), "W3": (128, "bfloat16"),
    "PI": (1, "int32"), "PA": (1, "int32"), "XC": (1, "float32"), "ZR": (256, "float32"), "LY": (16, "float32"), "KM": (16, "float32"),
    "KD": (32, "float32"), "DM": (1024, "bfloat16"), "ON16": (16, "float32"), "ZZ": (256, "bfloat16"),
    "D0": (528, "bfloat16"), "D1": (528, "bfloat16"), "D2": (1040, "bfloat16"), "D3": (1040, "bfloat16"), "D4": (1040, "float32"),
    "R": (3072, "bfloat16"), "RF": (1024, "float32"), "IN1": (4096, "bfloat16"), "X": (4096, "float32"),
    "NA": (64, "bfloat16"), "AR": (64, "float32"), "RR": (256, "float32"), "U01": (256, "bfloat16"), "UL": (16, "bfloat16"),
    "UK": (16, "float32"), "UK2": (16, "float32"), "CY": (16, "float32"), "SP": (16, "float32"), "OF": (16, "float32"), "OU": (16, "uint16"),
    "BS": (512, "bfloat16"), "BT": (256, "float32"), "BRF": (VL * 16, "float32"), "BRH": (4096 - VL * 16, "bfloat16"),
    "CLF0": (256, "float16"), "CLU0": (256, "uint16"), "CLF1": (256, "float16"), "CLU1": (256, "uint16"),
    "IN3": (VL * 16, "bfloat16"), "GA": (4096 - VL * 16, "bfloat16"), "SGN": (4096 - VL * 16, "bfloat16"),
    "L1": (16, "float32"), "L2": (16, "float32"), "LOST": (16, "float32"),
    "F": (256, "bfloat16"), "SM": (512, "float16"), "CR": (256, "float16"), "OKL": (16, "float32"), "OB": (16, "float32"),
    "CLM": (16, "float32"), "R2": (32, "float32"), "R3": (32, "float32"), "R4": (32, "float32"), "OFS": (32, "uint16"), "MLU": (16, "uint16"),
    "VB": (512, "float32"), "OV": (256, "float32"),
    "DL": (256, "bfloat16"), "ZF": (256, "float32"), "OFN": (256, "float32"), "OI": (256, "int32"), "EF": (256, "float32"), "YF": (256, "float32"),
}
SCRATCH = {k: ("sbuf", [128, n], d) for k, (n, d) in _sb.items()}
SCRATCH["E"] = ("sbuf", [128, 16, 256], "bfloat16")
SCRATCH["MK"] = ("sbuf", [128, 16, 16], "bfloat16")
SCRATCH["MD"] = ("sbuf", [128, 16, 16], "bfloat16")
for _t in range(3):
    SCRATCH["SW%d" % _t] = ("sbuf", [128, 512], "int32")
    SCRATCH["AV%d" % _t] = ("sbuf", [128, 64], "int32")
SCRATCH["TA"] = ("psum", [128, 1024], "float32")
SCRATCH["TB"] = ("psum", [128, 1024], "float32")
for _t in range(4, 8):
    SCRATCH["P%d" % _t] = ("psum", [128, 512], "float32")
PS = ("TA", "TB", "P4", "P5", "P6", "P7")
SEMAPHORES = ["cV", "cS", "cT", "cG"] + ["arr%d" % t for t in range(3)] + ["loc%d" % t for t in range(3)] + ["d%d" % k for k in range(8)]


def rank_program(g, core, T, topo):
    rank = T.rank_of(core)
    if rank is None:
        return
    queues = {"V": g.vector, "S": g.scalar, "T": g.tensor, "G": g, "Y": g.sync}
    count = {"cV": 0, "cS": 0, "cT": 0, "cG": 0}
    known = {q: {} for q in queues}
    clocks = {}
    log = {}
    nd = [0]
    hold = [None]

    def A(name, a=0, b=None, s=1):
        n = SCRATCH[name][1][1]
        b = n if b is None else b
        ap = T[name][:, a:b] if s == 1 else T[name][:, a:b:s]
        return (ap, [(name, a, b, s)])

    def ind(win, off):
        return (win[0].indirect(off[0]), win[1] + off[1])

    def keys(name, a, b, s=1):
        if name in PS:
            return [("%s.%d" % (name, k), 0, 512, 1, True) for k in range(a // 512, (b - 1) // 512 + 1)]
        return [(name, a, b, s, False)]

    def apart(a, b, s, x, y, z):
        return x >= b or y <= a or (s == z and s > 1 and (a - x) % s != 0)

    def need_event(q, ev):
        if known[q].get(ev[0], 0) >= ev[1]:
            return
        queues[q].wait_ge(T.sem[ev[0]], ev[1])
        k = known[q]
        for s, v in clocks.get(ev, {}).items():
            if k.get(s, 0) < v:
                k[s] = v
        if k.get(ev[0], 0) < ev[1]:
            k[ev[0]] = ev[1]

    def deps(q, reads, writes):
        out = {}
        for ops, w in ((reads, False), (writes, True)):
            for o in ops:
                for region in o[1]:
                    for key, lo, hi, st, bank in keys(*region):
                        for (x, y, ev, eq, ew, z) in log.get(key, []):
                            if apart(lo, hi, st, x, y, z) or (eq == q == "T" and bank):
                                continue
                            if (ew or w or (bank and eq != q)) and out.get(ev[0], 0) < ev[1]:
                                out[ev[0]] = ev[1]
        return out

    def record(q, ev, reads, writes):
        for ops, w in ((reads, False), (writes, True)):
            for o in ops:
                for region in o[1]:
                    for key, lo, hi, st, bank in keys(*region):
                        keep = []
                        for r in log.get(key, []):
                            inside = lo <= r[0] and r[1] <= hi and (st == 1 or (st == r[5] and (lo - r[0]) % st == 0))
                            if inside and r[3] == q and r[2][0] == ev[0] and (w or not r[4]):
                                continue
                            keep.append(r)
                        keep.append((lo, hi, ev, q, w, st))
                        log[key] = keep

    def waits(q, reads, writes):
        for s, v in sorted(deps(q, reads, writes).items(), key=lambda e: -e[1]):
            need_event(q, (s, v))

    def emit(q, fn, reads, writes):
        if hold[0] is not None:
            hold[0].append((q, fn, reads, writes))
            return
        waits(q, reads, writes)
        sem = "c" + q
        inst = fn()
        count[sem] += 1
        inst.then_inc(T.sem[sem], 1)
        ev = (sem, count[sem])
        clocks[ev] = dict(known[q])
        record(q, ev, reads, writes)

    def together(parts):
        if len(parts) == 1:
            return parts[0]()
        lists = []
        for f in parts:
            hold[0] = []
            f()
            units = []
            for call in hold[0]:
                if call[0] == "V" or not units:
                    units.append([])
                units[-1].append(call)
            lists.append(units)
        hold[0] = None
        while any(lists):
            for units in lists:
                if units:
                    for call in units.pop(0):
                        emit(*call)

    def dma(q, out, in_, reads, writes):
        waits(q, reads, writes)
        ev = ("d%d" % nd[0], 16)
        nd[0] += 1
        queues[q].dma_start(out, in_).then_inc(T.sem[ev[0]], 16)
        clocks[ev] = dict(known[q])
        record("dma%d" % nd[0], ev, reads, writes)
        return ev

    V, S, TE = g.vector, g.scalar, g.tensor

    def vts(out, i, s1, op0, s2=None, op1=None):
        rd = [i] + [s for s in (s1, s2) if isinstance(s, tuple)]
        a1 = s1[0] if isinstance(s1, tuple) else s1
        a2 = s2[0] if isinstance(s2, tuple) else s2
        if op1 is None:
            emit("V", lambda: V.tensor_scalar(out[0], i[0], a1, None, op0), rd, [out])
        else:
            emit("V", lambda: V.tensor_scalar(out[0], i[0], a1, a2, op0, op1), rd, [out])

    def vtt(out, i, j, op):
        emit("V", lambda: V.tensor_tensor(out[0], i[0], j[0], op), [i, j], [out])

    def vcp(out, i):
        emit("V", lambda: V.tensor_copy(out[0], i[0]), [i], [out])

    def vms(out, c):
        emit("V", lambda: V.memset(out[0], c), [], [out])

    def scan_(out, m, d, first):
        emit("V", lambda: V.tensor_tensor_scan(out[0], m[0], d[0], first, OP.mult, OP.add), [m, d], [out])

    def act(out, i, fn, bias=0.0, scale=1.0):
        if bias == 0.0 and scale == 1.0:
            emit("S", lambda: S.activation(out[0], i[0], fn), [i], [out])
        else:
            emit("S", lambda: S.activation(out[0], i[0], fn, bias=bias, scale=scale), [i], [out])

    def mm(out, l, r, start=True, stop=True):
        emit("T", lambda: TE.matmul(out[0], l[0], r[0], start, stop), [l, r], [out])

    def sel(out, i, pattern, op, fill, base, mult):
        emit("G", lambda: g.affine_select(out[0], i[0], pattern, op, fill, base, mult), [i], [out])

    def gcp(out, i, n):
        sel(out, i, [[0, n]], OP.is_ge, 0.0, 0, 0)

    def iota(out, pattern, base, mult, small=True):
        if small:
            emit("G", lambda: g.iota(out[0], pattern, base, mult, allow_small_or_imprecise_dtypes=True), [], [out])
        else:
            emit("G", lambda: g.iota(out[0], pattern, base, mult), [], [out])

    def EX(name, x):
        return A(name, 15 - x, 143 - x)

    def collect(out, name, rhs):
        for x in range(16):
            mm(out, EX(name, x), rhs(x), x == 0, x == 15)

    dma("S", T.OCN[:, :], T.occ[:, :], [], [A("OCN")])
    dma("S", T.CI[:, :], T.cards[:, :], [], [A("CI")])
    skills = dma("S", T.SK[:, :], T.skill[:, :], [], [A("SK")])
    dma("Y", T.ND[:, :], T.need[:, :], [], [A("ND")])
    need_event("Y", skills)
    dma("Y", T.COV[:, :], T.cover[:, :], [], [A("COV")])

    iota(A("PI"), [[0, 1]], 0, 1, False)
    vms(A("ONE"), 1.0)
    for z in ("Z0", "ZB", "Z8", "Z15"):
        vms(A(z), 0.0)
    vms(A("CM"), -1.0 / 16)
    sel(A("G8"), A("ONE", 0, 8), [[-16, 8]], OP.is_equal, 0.0, 0, 1)
    iota(A("ZR"), [[0, 16], [1, 16]], 0, 0)
    for k in range(4):
        sel(A("PX", 512 * k, 512 * k + 512), A("ONE"), [[-1, 4], [-16, 8], [0, 16]], OP.is_equal, 0.0, -4 * k, 1)
    iota(A("LY"), [[16, 16]], 0, 0)
    sel(A("G15"), A("ONE", 0, 8), [[-16, 8]], OP.is_equal, 0.0, -15, 1)
    sel(A("I"), A("ONE", 0, 128), [[-1, 128]], OP.is_equal, 0.0, 0, 1)
    sel(A("UN"), A("ONE", 0, 128), [[-16, 8], [0, 16]], OP.is_ge, 0.0, 0, 1)
    sel(A("B"), A("UN"), [[16, 8], [0, 16]], OP.is_ge, 0.0, 15, -1)
    sel(A("UP"), A("B"), [[-1, 128]], OP.is_gt, 0.0, 0, 1)
    for h in range(2):
        sel(A("DM", 512 * h, 512 * h + 512), A("ONE"), [[0, 32], [1, 16]], OP.is_gt, 0.0, 0, 0)
    sel(A("TRI"), A("B"), [[1, 128]], OP.is_gt, 0.0, 0, -1)
    iota(A("VB", 256, 512), [[0, 256]], 0, 0)
    iota(A("ON16"), [[0, 16]], 1, 0)
    iota(A("ZZ"), [[0, 256]], 0, 0)
    iota(A("NA"), [[0, 64]], 0, 0)
    for t in range(3):
        iota(A("SW%d" % t, 0, 64), [[0, 64]], 0, 0, False)
    vcp(A("Z0", 15, 143, 16), A("G8"))
    vts(A("Z8", 15, 143, 16), A("G8"), -8192.0, OP.mult)
    vts(A("PA"), A("PI"), 15, OP.bitwise_and)
    vcp(A("XC"), A("PA"))
    mk = (T.MK[:, :, :], [("MK", 0, 16)])
    for y in range(16):
        vts((T.MK[:, y, :], [("MK", y, y + 1)]), A("ZR", 0, 16), A("XC"), OP.is_gt)
    vts(A("OCH"), A("OCN"), -2048.0, OP.add)
    for k in range(8):
        ps, c = (("P6", 0), ("P7", 0), ("TA", 0), ("TA", 512), ("TB", 0), ("TB", 512), ("P4", 0), ("P6", 0))[k]
        for h in range(2):
            x = 2 * k + h
            mm(A(ps, c + 256 * h, c + 256 * h + 256), A("PX", 128 * x, 128 * x + 128), A("OCH"))
        if k % 2 == 0:
            vcp(A("OH", 512 * k, 512 * k + 512), A(ps, c, c + 512))
        else:
            act(A("OH", 512 * k, 512 * k + 512), A(ps, c, c + 512), FN.Copy)
    collect(A("P5", 0, 256), "Z0", lambda x: A("OH", x, 4096, 16))
    vts(A("CF"), A("CI"), -2048.0, OP.add)
    vcp(A("Z15", 15, 143, 16), A("G15"))
    collect(A("P7", 0, 64), "Z0", lambda x: A("CF", x, 1024, 16))
    collect(A("P7", 64, 128), "Z15", lambda x: A("CF", x, 1024, 16))
    vcp(A("CU"), A("CI"))
    vts(A("OLU"), A("P5", 0, 256), 2048.0, OP.add)
    vts(A("KD", 0, 16), A("LY"), A("XC"), OP.add)
    vts(A("KD", 16, 32), A("KD", 0, 16), 256.0, OP.add)
    vts(A("KM"), A("KD", 0, 16), 256.0, OP.add)
    vcp(A("ZB", 15, 143, 16), A("B", 0, 128, 16))
    vts(A("BB"), A("B"), 1048576.0, OP.mult)
    vts(A("ZH"), A("ZB"), 0.5, OP.mult)
    vts(A("NI"), A("I"), -1.0, OP.mult)
    vts(A("UM"), A("UP"), -1.0, OP.mult)
    sel(A("W3"), A("UM"), [[-1, 128]], OP.not_equal, 1000.0, 0, 1)
    vts(A("LS"), A("P7", 0, 128), 2048.0, OP.add)
    vts(A("KS"), A("LS", 0, 64), 512.0, OP.add)
    vts(A("NN"), A("ND"), -1024.0, OP.mult)
    vms(A("SK", 4095, 4096), -14.0 / 1024)
    for k in range(8):
        o, i = A("WA", 512 + 512 * k, 1024 + 512 * k), ind(A("SK"), A("OLU", 32 * k, 32 * k + 32))
        if k % 2 == 0:
            vts(o, i, 1024.0, OP.mult, float(K0), OP.add)
        else:
            act(o, i, FN.Identity, float(K0), 1024.0)

    def covers(t):
        f, u = "CLF%d" % (t % 2), "CLU%d" % (t % 2)
        vts(A(f), ind(A("COV"), A("LS", 16 * t, 16 * t + 16)), -2048.0, OP.add)
        vts(A(u), A(f), 2048.0, OP.add)

    def moved():
        act(ind(A("OO"), A("OFS", 0, 16)), A("OV"), FN.Silu)

    win = ["WA", "WB"]
    for t in range(4):
        W, N = win[t % 2], win[1 - t % 2]
        wst, nst = A(W, 512, 4608), A(N, 512, 4608)
        clf, clu = "CLF%d" % (t % 2), "CLU%d" % (t % 2)
        brep = [(A("BRF", i, VL * 16, 16), A("BT", 0, VL), VL) for i in range(16)]
        brep += [(A("BRH", i, 4096 - VL * 16, 16), A("BS", VL, 256), 256 - VL) for i in range(16)]

        def Dc(c, a, b, s=1):
            return A("D%d" % c, a, b, s)

        def own(k):
            if k == 0:
                act(A("BS", 256, 512), ind(wst, A("LS", 64 + 16 * t, 80 + 16 * t)), FN.Copy)
                return
            act(A("BS", 0, 256), ind(wst, A("LS", 16 * t, 16 * t + 16)), FN.Copy)
            act(A("BT"), A("BS", 0, 256), FN.Identity, -float(TOL))

        def gather(c, q):
            l0, n = CH[c]
            o, i = Dc(c, 1, 1 + 16 * n), ind(wst, A("CU", 256 * t + l0, 256 * t + l0 + n))
            if q == "V":
                vcp(o, i)
            else:
                act(o, i, FN.Copy)

        def repeat(k):
            for j in range(k):
                o, i, m = brep.pop(0)
                gcp(o, i, m)

        def psum(c, a, b, s=1):
            name, off = (("TA", 0), ("TA", 512), ("TB", 0), ("TA", 0), ("TB", 0))[c]
            return A(name, off + a, off + b, s)

        def scan(c):
            l0, n = CH[c]
            if c < 4:
                vcp(Dc(c, 0, 16 * n, 16), A("NN", 192 * t + l0, 192 * t + l0 + n))
            elif t:
                ev = ("arr%d" % (t - 1), len(topo.engines(T.cores[rank - 1], core)))
                record("net", ev, [], [A("AV%d" % (t - 1))])
                vts(Dc(4, 0, 1024, 16), A("AV%d" % (t - 1)), -1024.0, OP.mult)
                vts(A("NA"), A("AV%d" % (t - 1)), -1024.0, OP.mult)
            else:
                vms(Dc(4, 0, 1024, 16), 0.0)
            r = A("R", 16 * l0, 16 * l0 + 16 * n) if c < 4 else A("RF")
            scan_(r, A("DM", 0, 16 * n), Dc(c, 0, 16 * n), 0.0)
            vts(A("IN1", 16 * l0, 16 * l0 + 16 * n), r, -512.0, OP.is_ge, -15.5 / 16, OP.add)
            for k in range(n // 32):
                mm(psum(c, 512 * k, 512 * k + 512), A("BB"), A("IN1", 16 * l0 + 512 * k, 16 * l0 + 512 * k + 512))

        def total(c):
            l0, n = CH[c]
            if t < 3:
                for p in range(16):
                    mm(A("P4", l0, l0 + n), A("I"), Dc(c, p, 16 * n, 16), p == 0, False)
                mm(A("P4", l0, l0 + n), A("I"), A("BS", 256 + l0, 256 + l0 + n), False, True)

        def leave(c):
            l0, n = CH[c]
            vtt(A("X", 16 * l0, 16 * l0 + 16 * n), Dc(c, 1, 1 + 16 * n), psum(c, 0, 16 * n), OP.min)
            vtt(A("X", 16 * l0 + 15, 16 * l0 + 16 * n, 16), A("BS", 256 + l0, 256 + l0 + n), psum(c, 15, 16 * n, 16), OP.min)
            act(ind(nst, A("CU", 256 * t + l0, 256 * t + l0 + n)), A("X", 16 * l0, 16 * l0 + 16 * n), FN.Silu)

        def lost(k):
            if k == 0:
                collect(A("P5", 256, 268), "ZB", lambda x: A("NN", 192 * t + x, 192 * t + 192, 16))
                collect(A("P5", 272, 288), "ZB", lambda x: A("BS", x, 256, 16))
            else:
                collect(A("P5", 268, 272), "ZB", lambda x: A("NA", x, 64, 16))

        def rest(c):
            if t < 3:
                vtt(A("AR"), A("RF", 15, 1024, 16), A("BS", 448, 512), OP.add)
                vts(A("RR", 192, 256), A("AR"), -1.0 / 1024, OP.mult, 0.0, OP.max)

        def rest2(c):
            if t < 3:
                vts(A("RR", 0, 192), A("P4", 0, 192), -1.0 / 1024, OP.mult, 0.0, OP.max)
                vts(A("U01"), A("RR"), 0.5, OP.is_gt)

        def run(order, do):
            for step in order.split():
                together([(lambda s=s: do[s[0]](int(s[1:]))) for s in step.split("+")])

        run(STEP1, {"v": lambda c: gather(c, "V"), "a": lambda c: gather(c, "S"), "b": own, "r": repeat, "s": scan, "t": total,
                    "l": leave, "q": lost, "x": rest, "y": rest2})
        if t == 0:
            covers(0)

        def unmet(c):
            if t < 3:
                collect(A("P5", 0, 16), "ZB", lambda x: A("U01", x, 256, 16))

        def lost2(c):
            vts(A("L1"), A("P5", 256, 272), -512.0, OP.is_lt)
            vts(A("L2"), A("P5", 272, 288), float(TOL), OP.is_ge)
            vtt(A("LOST"), A("L1"), A("L2"), OP.mult)

        def slots(c):
            if t < 3:
                vts(A("UL"), A("P5", 0, 16), 0.5, OP.is_ge)
                vts(A("UK"), A("P5", 0, 16), 0.5, OP.is_lt)
                mm(A("P5", 16, 32), A("B"), A("UL"))
                mm(A("P5", 32, 48), A("W3"), A("UL"))

        def slots2(c):
            if t < 3:
                vtt(A("UK2"), A("UK"), A("KM"), OP.mult)
                scan_(A("CY"), A("ON16"), A("P5", 16, 32), -1001.0)
                vtt(A("SP"), A("P5", 32, 48), A("CY"), OP.add)
                vtt(A("OF"), A("SP"), A("UK2"), OP.max)
                vcp(A("OU"), A("OF"))

        def slots3(c):
            if t < 3:
                vcp(ind(A("SW%d" % t), A("OU")), A("RR"))

        def spsum(k):
            return A(*(("TA", 0, 512), ("TA", 512, 1024), ("TB", 0, 16 * SG3[2][1]))[k])

        def sgather(k):
            l0, n = SG3[k]
            ga, br = A("GA", 16 * (l0 - VL), 16 * (l0 - VL + n)), A("BRH", 16 * (l0 - VL), 16 * (l0 - VL + n))
            act(ga, ind(nst, A(clu, l0, l0 + n)), FN.Copy)
            mm(spsum(k), A("NI"), br, True, False)
            mm(spsum(k), A("I"), ga, False, True)

        def ssign(k):
            l0, n = SG3[k]
            act(A("SGN", 16 * (l0 - VL), 16 * (l0 - VL + n)), spsum(k), FN.Sign, float(TOL))

        def fused(k):
            l0, n = FG[k]
            vtt(A("IN3", 16 * l0, 16 * (l0 + n)), ind(nst, A(clu, l0, l0 + n)), A("BRF", 16 * l0, 16 * (l0 + n)), OP.is_ge)

        def counts(k):
            for i in range(16):
                if k == 0 or k == 3:
                    h = 64 if k else 0
                    mm(A("P6", h, h + 64), EX("ZB", i), A("IN3", 16 * h + i, 16 * h + 1024, 16), i == 0, i == 15)
                elif k == 1:
                    mm(A("P4", 0, VL - 128), EX("ZB", i), A("IN3", 2048 + i, VL * 16, 16), i == 0, False)
                else:
                    a, b = ((0, 64), (64, 256 - VL))[k == 4]
                    mm(A("P4", VL - 128 + a, VL - 128 + b), EX("ZH", i), A("SGN", 16 * a + i, 16 * b, 16), i == 0, i == 15)
            if k == 1:
                mm(A("P4", 0, VL - 128), A("CM"), A("ONE", 0, VL - 128), False, True)

        def fits(k):
            p, l0, n = PART[k]
            vts(A("F", l0, l0 + n), A(p, 0, n), (8.5, 0.5)[k], OP.is_ge)
            mm(A(p, 256, 256 + n), A("TRI"), A("F", l0, l0 + n))

        def first(k):
            p, l0, n = PART[k]
            vtt(A("SM", 256 + l0, 256 + l0 + n), A("F", l0, l0 + n), A(p, 256, 256 + n), OP.is_gt)
            vtt(A("SM", l0, l0 + n), A("SM", 256 + l0, 256 + l0 + n), A(clf, l0, l0 + n), OP.mult)

        def covers_next(c):
            if t < 3:
                covers(t + 1)

        def moved_before(c):
            if t:
                moved()

        run(STEP3, {"u": unmet, "g": sgather, "s": ssign, "v": fused, "c": counts, "f": fits, "o": first, "L": lost2, "p": slots,
                    "P": slots2, "Q": slots3, "m": moved_before, "C": covers_next})
        mm(A("P4", 0, 256), A("B"), A("SM", 0, 256))
        collect(A("P5", 64, 96), "ZB", lambda x: A("SM", x, 512, 16))
        act(A("CR"), A("P4", 0, 256), FN.Copy)
        vtt(A("OKL"), A("P5", 80, 96), A("LOST"), OP.mult)
        vts(A("MLU"), A("P5", 64, 80), 2048.0, OP.add)
        act(A("VB", 0, 256), ind(nst, A("MLU")), FN.Copy)
        if t == 0:
            act(A("OO", 512, 4608), A("OH"), FN.Silu, 2080.0)
        act(A("OV"), ind(A("OO", 512, 4608), A("MLU")), FN.Copy)
        mm(A("P4", 0, 256), A("B"), A("ZZ"), True, False)
        for y in range(16):
            ey = (T.E[:, y, 0:256 - 16 * y], [("E", 256 * y, 256 * y + 256)])
            vts(ey, A("CR", 16 * y, 256), A("P5", 64 + y, 65 + y), OP.is_equal, A("OKL", y, y + 1), OP.mult)
            if y < 15:
                mm(A("P4", 16 * y + 16, 256), A("B"), (T.E[:, y, 16:256 - 16 * y], ey[1]), False, False)
        md = (T.MD[:, :, :], [("MD", 0, 16)])
        vtt(md, (T.E[:, :, 0:16], [("E", 0, 4096)]), mk, OP.mult)
        mm(A("P4", 0, 256), A("B"), md, False, True)
        vts(A("OB"), A("OKL"), 8192.0, OP.mult, -8192.0, OP.add)
        vts(A("CLM"), A("P5", 64, 80), 2560.0, OP.add)
        vtt(A("R2", 0, 16), A("OB"), A("KS", 16 * t, 16 * t + 16), OP.add)
        vtt(A("R2", 16, 32), A("OB"), A("CLM"), OP.add)
        vcp(A("DL"), A("P4", 0, 256))
        collect(A("P5", 128, 144), "Z8", lambda x: A("DL", x, 256, 16))
        if t < 3:
            dst = T.cores[(rank + 1) % len(T.cores)]
            addr = topo.addr(dst)
            src = A("SW%d" % t, 0, 64)
            waits("G", [src], [])
            g.remote_dma(out_ap=T["AV%d" % t][:, :], in_ap=src[0], remote_sem=T.sem["arr%d" % t], local_sem=T.sem["loc%d" % t],
                         pid=addr[1], routing_id=addr[0], dma_engine_mask=topo.mask(core, dst))
        vtt(A("R3", 0, 16), A("P5", 128, 144), A("R2", 0, 16), OP.add)
        vtt(A("R3", 16, 32), A("P5", 128, 144), A("R2", 16, 32), OP.add)
        vtt(A("R4"), A("R3"), A("KD"), OP.max)
        vcp(A("OFS"), A("R4"))
        vcp(ind(A(N), A("OFS")), A("VB"))
    moved()
    dma("Y", T.ZF[:, :], T.WA[0:128:16, 512:4608], [A("WA", 512, 4608)], [A("ZF")])
    dma("Y", T.OFN[:, :], T.OO[0:128:16, 512:4608], [A("OO", 512, 4608)], [A("OFN")])
    vts(A("EF"), A("ZF"), float(TOL), OP.is_lt, 4095.0, OP.mult)
    vts(A("OI"), A("OFN"), -32.0, OP.add)
    vtt(A("YF"), A("OI"), A("EF"), OP.max)
    need_event("Y", dma("Y", T.y[:, :], T.YF[:, :], [A("YF")], []))
    for t in range(3):
        g.wait_ge(T.sem["loc%d" % t], len(topo.engines(core, T.cores[(rank + 1) % len(T.cores)])))
    for s in ("cV", "cS", "cT", "cG"):
        need_event("G", (s, count[s]))
